import numpy as np
import ml_dtypes


def mxq(x, axis, fmt="e4m3"):
    dtype, down = {"e4m3": (ml_dtypes.float8_e4m3fn, 7), "e5m2": (ml_dtypes.float8_e5m2, 14)}[fmt]
    v = np.moveaxis(np.asarray(x, np.float32).astype(ml_dtypes.bfloat16).astype(np.float64), axis, -1)
    blocks = v.reshape(v.shape[:-1] + (-1, 32))
    amax = np.abs(blocks).max(-1, keepdims=True)
    byte = np.maximum(np.where(amax > 0, np.frexp(amax)[1] - 1 + 127, 0) - down, 1)
    scale = np.exp2(byte - 127.0)
    codes = (blocks / scale).astype(np.float32).astype(dtype).astype(np.float64)
    return np.moveaxis((codes * scale).reshape(v.shape), -1, axis)


WIDE = False


def mx_kscale(k):
    if not WIDE:
        return np.ones(k)
    levels = np.array([10, -10, 5, -5, 0])
    if k % 512:
        return np.exp2(np.random.permutation(np.resize(levels, k // 32))).repeat(32)
    a = np.empty((k // 512, 16))
    for p in range(k // 512):
        a[p, :8] = np.random.permutation(np.resize(levels, 8))
        for g in range(8):
            far = levels[np.abs(levels - a[p, g]) >= 10]
            a[p, g + 8] = far[np.random.randint(len(far))]
    return np.exp2(a.ravel()).repeat(32)


BF16 = ml_dtypes.bfloat16


def bf(x):
    return np.asarray(x, np.float32).astype(BF16)


def f64(x):
    return np.asarray(x).astype(np.float64)


E2M1 = np.array([0.0, 0.5, 1.0, 1.5, 2.0, 3.0, 4.0, 6.0, -0.0, -0.5, -1.0, -1.5, -2.0, -3.0, -4.0, -6.0])


def pack_weight(w, fmt):
    k, n = w.shape
    w = f64(bf(w)).reshape(k // 32, 32, n)
    amax = np.abs(w).max(1)
    if fmt == "e4m3":
        byte = np.frexp(amax)[1] - 1 + 127 - 7
    else:
        mant, ex = np.frexp(amax / 6.0)
        byte = np.where(mant > 0.5, ex, ex - 1) + 127
    byte = np.clip(np.where(amax > 0, byte, 1), 1, 254)
    scaled = (w * np.exp2(127.0 - byte)[:, None, :]).reshape(k, n).astype(np.float32)
    by_word = np.ascontiguousarray(scaled.reshape(k // 512, 128, 4, n).transpose(0, 1, 3, 2))
    if fmt == "e4m3":
        words = by_word.astype(ml_dtypes.float8_e4m3fn).view(np.uint8)
    else:
        c = by_word.astype(ml_dtypes.float4_e2m1fn).view(np.uint8) & 0xF
        words = c[..., 0::2] | (c[..., 1::2] << 4)
    return np.ascontiguousarray(words), np.ascontiguousarray(byte.astype(np.uint8).reshape(k // 512, 16, n))


def unpack_weight(words, scales, fmt):
    g, p, n, _ = words.shape
    if fmt == "e4m3":
        vals = np.ascontiguousarray(words).view(ml_dtypes.float8_e4m3fn).astype(np.float64)
    else:
        nib = np.empty((g, p, n, 4), np.uint8)
        nib[..., 0::2] = words & 0xF
        nib[..., 1::2] = words >> 4
        vals = E2M1[nib]
    vals = vals * np.repeat(np.exp2(scales.astype(np.float64) - 127.0), 8, axis=1)[..., None]
    return vals.transpose(0, 1, 3, 2).reshape(g * 512, n)
def pack4(w):
    words, scales = pack_weight(w, "e2m1")
    return words.reshape(words.shape[0], 128, -1), scales


def unpack4(words, scales):
    return unpack_weight(words.reshape(words.shape[0], 128, -1, 2), scales, "e2m1")


def planes(Y):
    n, m = Y.shape
    b = f64(bf(Y)).reshape(n // 32, 32, m)
    amax = np.abs(b).max(1)
    byte = np.clip(np.where(amax > 0, np.frexp(amax)[1] - 1 + 127 - 7, 1), 1, 254)
    codes = (b * np.exp2(127.0 - byte)[:, None, :]).reshape(n, m).astype(np.float32).astype(ml_dtypes.float8_e4m3fn).view(np.uint8)
    words = codes.reshape(n // 512, 128, 4, m).transpose(0, 1, 3, 2)
    return np.ascontiguousarray(words), np.ascontiguousarray(byte.astype(np.uint8).reshape(n // 512, 16, m))


T, KA, KP, G, N, XY = 2048, 512, 1024, 1024, 512, 2

def deviations(k, points):
    tx, rx = 1.5 * np.random.randn(k, XY), 1.5 * np.random.randn(k, XY)
    out = np.sqrt(((tx[:, None, :] - points[None]) ** 2).sum(-1))
    back = np.sqrt(((rx[:, None, :] - points[None]) ** 2).sum(-1))
    r2 = (out + back) ** 2
    return (r2 - r2.mean(1, keepdims=True)) / r2.std(1, keepdims=True)

def setup_inputs():
    points = np.random.uniform(-1.0, 1.0, (G + T, XY))
    da, dp = deviations(KA, points), deviations(KP, points)
    energy = np.sqrt((da[:, :G] ** 2).sum(0) + (dp[:, :G] ** 2).sum(0))
    sa, sp, t = mx_kscale(KA), mx_kscale(KP), mx_kscale(G)
    za = 2.0 * da[:, G:].T / np.sqrt(KA + KP) + np.random.randn(T, KA)
    zp = 2.0 * dp[:, G:].T / np.sqrt(KA + KP) + np.random.randn(T, KP)
    passive_words, passive_scales = pack4(dp[:, :G] / energy / sp[:, None])
    fuse = 1.5 * np.random.randn(G, N) / np.sqrt(G)
    fuse_words, fuse_scales = pack_weight(fuse / t[:, None], "e4m3")
    gain = np.exp(0.8 * np.random.randn(N))
    return {
        "za": bf(za * sa), "da": bf(da[:, :G] / energy / sa[:, None]),
        "zp": bf(zp * sp), "passive_words": passive_words, "passive_scales": passive_scales,
        "cell_weight": bf(np.exp(0.3 * np.random.randn(G)) * t),
        "fuse_words": fuse_words, "fuse_scales": fuse_scales,
        "zone_gain": bf(gain), "fade": bf(np.random.uniform(0.3, 0.9, N)),
        "prev": bf(np.random.randn(T, N) * gain), "bias": bf(0.3 * np.random.randn(N) * gain),
    }

def reference(za, da, zp, passive_words, passive_scales, cell_weight, fuse_words, fuse_scales, zone_gain, fade, prev, bias):
    active = mxq(f64(za), 1) @ mxq(f64(da), 0)
    passive = mxq(f64(zp), 1) @ unpack4(passive_words, passive_scales)
    h = np.tanh(active + passive) * f64(cell_weight)
    fused = mxq(h, 1) @ unpack_weight(fuse_words, fuse_scales, "e4m3")
    y = f64(zone_gain) * fused + f64(fade) * f64(prev) + f64(bias)
    Y = y.T
    words, scales = planes(Y)
    return y, words, scales

@@ -1,0 +1,586 @@
+from contextlib import ExitStack
+
+import concourse.mybir as mybir
+from concourse.masks import make_identity
+
+T, KA, KP, G, N = 2048, 512, 1024, 1024, 512
+FLOPS = 2 * T * G * (KA + KP) + 2 * T * G * N
+
+F32 = mybir.dt.float32
+BF16 = mybir.dt.bfloat16
+I32 = mybir.dt.int32
+U32 = mybir.dt.uint32
+U8 = mybir.dt.uint8
+FP8X4 = mybir.dt.float8_e4m3fn_x4
+FP4X4 = mybir.dt.float4_e2m1fn_x4
+ACT = mybir.ActivationFunctionType
+ALU = mybir.AluOpType
+
+P = 128
+PACK = 4
+KPASS = P * PACK
+CH = 512
+NCH = T // CH
+TT = CH // P
+BANKS = 8
+
+
+def tile_multistatic_range_fusion_k6_kernel(
+    tc, za, da, zp, passive_words, passive_scales, cell_weight, fuse_words, fuse_scales,
+    zone_gain, fade, prev, bias, out_0, out_1, out_2,
+):
+    nc = tc.nc
+    with ExitStack() as ctx:
+        keep = ctx.enter_context(tc.tile_pool(name="keep", bufs=1))
+        psum = ctx.enter_context(tc.psum_pool(name="psum", bufs=1))
+        ctx.enter_context(tc.manual_schedule())
+
+        turns = {}
+
+        def ring(name, depth, shape, dtype):
+            turn = turns.get(name, 0)
+            turns[name] = turn + 1
+            return keep.tile(shape, dtype, name=name, tag="%s%d" % (name, turn % depth), align_bytes=64)
+
+        def held(name, shape, dtype):
+            return keep.tile(shape, dtype, name=name, tag=name, align_bytes=64)
+
+        def bank():
+            turn = turns.get("bank", 0)
+            turns["bank"] = turn + 1
+            return psum.tile([P, CH], F32, name="bank", tag="bank%d" % (turn % BANKS))
+
+        scale_raw = held("scale_raw", [P, 2, G], U8)
+        nc.vector.memset(scale_raw[:].rearrange("p g n -> p (g n)").bitcast(I32), 0)
+        w_scale_raw = held("w_scale_raw", [P, 2, N], U8)
+        nc.vector.memset(w_scale_raw[:].rearrange("p g n -> p (g n)").bitcast(I32), 0)
+        warm = held("warm", [P, 8], F32)
+        nc.vector.memset(warm[:], 0.0)
+        warm_out = held("warm_out", [P, 8], F32)
+        ident = held("ident", [P, P], F32)
+        make_identity(nc, ident[:])
+
+        for q in range(4):
+            nc.scalar.dma_start(
+                out=scale_raw[32 * q : 32 * q + 4, :, :].bitcast(I32),
+                in_=passive_scales[:, 4 * q : 4 * q + 4, :].rearrange("g r n -> r g n").bitcast(I32),
+            )
+        nc.scalar.activation(out=warm_out[:], in_=warm[:], func=ACT.Tanh)
+
+        dp_raw, da_raw, z_raw, prev_raw = {}, {}, {}, {}
+
+        def load_dp(h):
+            dp_raw[h] = held("dp_raw%d" % h, [P, 2, 2 * KPASS], U8)
+            nc.sync.dma_start(
+                out=dp_raw[h][:].bitcast(I32),
+                in_=passive_words[:, :, 2 * KPASS * h : 2 * KPASS * (h + 1)].rearrange("g p n -> p g n").bitcast(I32),
+            )
+
+        def load_da(h):
+            da_raw[h] = held("da_raw%d" % h, [P, PACK, KPASS], BF16)
+            nc.sync.dma_start(
+                out=da_raw[h][:], in_=da[:, KPASS * h : KPASS * (h + 1)].rearrange("(p j) c -> p j c", j=PACK)
+            )
+
+        def load_z(c, g, pieces=1):
+            src = zp[:, KPASS * g : KPASS * (g + 1)] if g < 2 else za
+            z_raw[c, g] = held("z_raw%d_%d" % (c, g), [P, TT, KPASS], BF16)
+            rows = src[CH * c : CH * (c + 1), :].rearrange("(a p) k -> p a k", p=P)
+            step = TT // pieces
+            for a in range(0, TT, step):
+                nc.sync.dma_start(out=z_raw[c, g][:, a : a + step, :], in_=rows[:, a : a + step, :])
+
+        def load_prev(c):
+            prev_raw[c] = held("prev_raw%d" % c, [P, TT, N], BF16)
+            nc.sync.dma_start(
+                out=prev_raw[c][:], in_=prev[CH * c : CH * (c + 1), :].rearrange("(a p) k -> p a k", p=P)
+            )
+
+        cw = held("cw", [P, 2, PACK], BF16)
+        nc.gpsimd.dma_start(out=cw[:], in_=cell_weight.rearrange("(h p t) -> p h t", h=2, t=PACK))
+        vec = {}
+        for name, src in (("fade", fade), ("bias", bias), ("gain", zone_gain)):
+            vec[name] = held(name, [P, PACK], BF16)
+            nc.gpsimd.dma_start(out=vec[name][:], in_=src.rearrange("(p t) -> p t", t=PACK))
+        fade32 = held("fade32", [P, PACK], F32)
+
+        load_z(0, 0)
+        load_dp(0)
+        load_z(0, 1)
+        load_z(0, 2)
+        load_da(0)
+        load_dp(1)
+        load_da(1)
+        for g in range(3):
+            load_z(1, g)
+        load_prev(0)
+        w_raw = held("w_raw", [P, 2, N], U32)
+        nc.sync.dma_start(out=w_raw[:].bitcast(I32), in_=fuse_words.rearrange("g p n t -> p g (n t)").bitcast(I32))
+        for q in range(4):
+            nc.sync.dma_start(
+                out=w_scale_raw[32 * q : 32 * q + 4, :, :].bitcast(I32),
+                in_=fuse_scales[:, 4 * q : 4 * q + 4, :].rearrange("g r n -> r g n").bitcast(I32),
+            )
+        for c in range(2, NCH):
+            for g in range(3):
+                load_z(c, g)
+            load_prev(c - 1)
+        load_prev(NCH - 1)
+
+        dp_codes, dp_scales, da_grouped, da_codes, da_scales = {}, {}, {}, {}, {}
+
+        def order_dp(h):
+            dp_codes[h] = held("dp_codes%d" % h, [P, 2, 2 * KPASS], U8)
+            for g in range(2):
+                nc.vector.tensor_copy(
+                    out=dp_codes[h][:, g, :].rearrange("p (t m b) -> p t m b", t=PACK, b=2),
+                    in_=dp_raw[h][:, g, :].rearrange("p (m t b) -> p t m b", t=PACK, b=2),
+                )
+
+        def order_scales(h):
+            dp_scales[h] = held("dp_scales%d" % h, [P, 2, KPASS], U8)
+            nc.vector.tensor_copy(
+                out=dp_scales[h][:].rearrange("p g (t m) -> p g t m", t=PACK),
+                in_=scale_raw[:, :, KPASS * h : KPASS * (h + 1)].rearrange("p g (m t) -> p g t m", t=PACK),
+            )
+
+        def group_da(h, copy):
+            da_grouped[h] = ring("h_grouped", 2, [P, PACK * CH], BF16)
+            copy(
+                out=da_grouped[h][:].rearrange("p (t m j) -> p t m j", t=PACK, j=PACK),
+                in_=da_raw[h][:].rearrange("p j (m t) -> p t m j", t=PACK),
+            )
+
+        def quantize_da(h):
+            da_codes[h] = held("da_codes%d" % h, [P, KPASS], U32)
+            da_scales[h] = held("da_scales%d" % h, [P, KPASS], U8)
+            nc.vector.quantize_mx(out=da_codes[h][:].bitcast(FP8X4), scales=da_scales[h][:], in_=da_grouped[h][:])
+
+        w_codes = held("w_codes", [P, 2, N], U32)
+
+        w_scales = held("w_scales", [P, 2, N], U8)
+
+        def order_w_scales():
+            nc.vector.tensor_copy(
+                out=w_scales[:].rearrange("p g (t m) -> p g t m", t=PACK),
+                in_=w_scale_raw[:].rearrange("p g (m t) -> p g t m", t=PACK),
+            )
+
+        def order_w():
+            nc.vector.tensor_copy(
+                out=w_codes[:].bitcast(I32).rearrange("p g (t m) -> p g t m", t=PACK),
+                in_=w_raw[:].bitcast(I32).rearrange("p g (m t) -> p g t m", t=PACK),
+            )
+
+        z_banks, z_grouped, z_codes, z_scales = {}, {}, {}, {}
+
+        def turn_z(c, g):
+            words = z_raw[c, g][:].bitcast(F32)
+            for half in range(2):
+                z_banks[c, g, half] = bank()
+                for a in range(2):
+                    for u in range(2):
+                        col = 2 * P * u + P * a
+                        nc.tensor.transpose(
+                            z_banks[c, g, half][:, col : col + P], words[:, 2 * half + a, u :: 2], ident[:]
+                        )
+
+        def turn_z_half(c, g, half):
+            words = z_raw[c, g][:].bitcast(F32)
+            z_banks[c, g, half] = bank()
+            for a in range(2):
+                for u in range(2):
+                    col = 2 * P * u + P * a
+                    nc.tensor.transpose(z_banks[c, g, half][:, col : col + P], words[:, 2 * half + a, u :: 2], ident[:])
+
+        def copy_z(c, g, half):
+            if half == 0:
+                z_grouped[c, g] = ring("bf_stage", 4, [P, PACK * CH], BF16)
+            dst = z_grouped[c, g][:].bitcast(F32)[:, CH * half : CH * (half + 1)]
+            nc.scalar.copy(
+                out=dst.rearrange("p (n u) -> p n u", u=2),
+                in_=z_banks[c, g, half][:].rearrange("p (u n) -> p n u", u=2),
+            )
+
+        def quantize_z(c, g, lo=0, hi=CH):
+            if lo == 0:
+                z_codes[c, g] = ring("z_codes", 6, [P, CH], U32)
+                z_scales[c, g] = ring("z_scales", 6, [P, CH], U8)
+            nc.vector.quantize_mx(
+                out=z_codes[c, g][:, lo:hi].bitcast(FP8X4), scales=z_scales[c, g][:, lo:hi],
+                in_=z_grouped[c, g][:, PACK * lo : PACK * hi],
+            )
+
+        s_banks, th, h_grouped, h_codes, h_scales = {}, {}, {}, {}, {}
+
+        def correlate_pass(c, h, t, g):
+            if g == 0:
+                s_banks[c, h, t] = bank()
+            cols = slice(P * t, P * (t + 1))
+            if g < 2:
+                lhsT = dp_codes[h][:, g, 2 * P * t : 2 * P * (t + 1)].bitcast(FP4X4)
+                lhsT_scale = dp_scales[h][:, g, cols]
+            else:
+                lhsT = da_codes[h][:, cols].bitcast(FP8X4)
+                lhsT_scale = da_scales[h][:, cols]
+            nc.tensor.matmul_mx(
+                out=s_banks[c, h, t][:], lhsT=lhsT, lhsT_scale=lhsT_scale,
+                rhs=z_codes[c, g][:].bitcast(FP8X4), rhs_scale=z_scales[c, g][:],
+                start=(g == 0), stop=(g == 2),
+            )
+
+        def correlate_group(c, h, t):
+            for g in range(3):
+                correlate_pass(c, h, t, g)
+
+        def correlate(c, h):
+            for t in range(PACK):
+                for g in range(3):
+                    correlate_pass(c, h, t, g)
+
+        def squash(c, h, t):
+            if t == 0:
+                th[c, h] = ring("th", 2, [P, PACK, CH], F32)
+            nc.scalar.activation(out=th[c, h][:, t, :], in_=s_banks[c, h, t][:], func=ACT.Tanh)
+
+        def weigh(c, h):
+            h_grouped[c, h] = ring("h_grouped", 2, [P, PACK * CH], BF16)
+            nc.vector.tensor_tensor(
+                out=h_grouped[c, h][:].rearrange("p (n t) -> p n t", t=PACK),
+                in0=th[c, h][:].rearrange("p t n -> p n t"),
+                in1=cw[:, h, :].unsqueeze(1).to_broadcast([P, CH, PACK]),
+                op=ALU.mult,
+            )
+
+        def quantize_h(c, h):
+            h_codes[c, h] = ring("h_codes", 4, [P, CH], U32)
+            h_scales[c, h] = ring("h_scales", 4, [P, CH], U8)
+            nc.vector.quantize_mx(out=h_codes[c, h][:].bitcast(FP8X4), scales=h_scales[c, h][:], in_=h_grouped[c, h][:])
+
+        prev_banks, faded, f_banks, y_zones = {}, {}, {}, {}
+
+        def turn_prev(c):
+            words = prev_raw[c][:].bitcast(F32)
+            for u in range(2):
+                prev_banks[c, u] = bank()
+                for a in range(TT):
+                    nc.tensor.transpose(prev_banks[c, u][:, P * a : P * (a + 1)], words[:, a, u :: 2], ident[:])
+
+        def turn_prev_half(c, u):
+            words = prev_raw[c][:].bitcast(F32)
+            prev_banks[c, u] = bank()
+            for a in range(TT):
+                nc.tensor.transpose(prev_banks[c, u][:, P * a : P * (a + 1)], words[:, a, u :: 2], ident[:])
+
+        def fade_prev(c, t):
+            if t == 0:
+                faded[c] = ring("faded", 2, [P, PACK, CH], F32)
+            pair = prev_banks[c, t // 2][:].bitcast(BF16).rearrange("p (n e) -> p e n", e=2)
+            nc.scalar.activation(
+                out=faded[c][:, t, :], in_=pair[:, t % 2, :], func=ACT.Identity,
+                scale=fade32[:, t : t + 1], bias=vec["bias"][:, t : t + 1],
+            )
+
+        def fuse_pass(c, t, h):
+            if h == 0:
+                f_banks[c, t] = bank()
+            cols = slice(P * t, P * (t + 1))
+            nc.tensor.matmul_mx(
+                out=f_banks[c, t][:], lhsT=w_codes[:, h, cols].bitcast(FP8X4), lhsT_scale=w_scales[:, h, cols],
+                rhs=h_codes[c, h][:].bitcast(FP8X4), rhs_scale=h_scales[c, h][:],
+                start=(h == 0), stop=(h == 1),
+            )
+
+        def fuse_group(c, t):
+            for h in range(2):
+                fuse_pass(c, t, h)
+
+        def fuse(c):
+            for t in range(PACK):
+                for h in range(2):
+                    fuse_pass(c, t, h)
+
+        def join(c, t):
+            if t == 0:
+                y_zones[c] = ring("y_zones", 2, [P, PACK, CH], F32)
+            nc.vector.scalar_tensor_tensor(
+                out=y_zones[c][:, t, :], in0=f_banks[c, t][:], scalar=vec["gain"][:, t : t + 1],
+                in1=faded[c][:, t, :], op0=ALU.mult, op1=ALU.add,
+            )
+
+        y_banks, y_rows, y_grouped = {}, {}, {}
+        y_codes = held("y_codes", [P, T], U32)
+        y_scales = held("y_scales", [P, T], U8)
+
+        def turn_y_tile(c, a):
+            y_banks[c, a] = bank()
+            for t in range(PACK):
+                nc.tensor.transpose(
+                    y_banks[c, a][:, P * t : P * (t + 1)], y_zones[c][:, t, P * a : P * (a + 1)], ident[:]
+                )
+
+        def turn_y(c):
+            for a in range(TT):
+                turn_y_tile(c, a)
+
+        def copy_y(c, a, engine):
+            y_rows[c, a] = ring("y_rows", 6, [P, N], F32)
+            dst = y_rows[c, a][:].rearrange("q (p t) -> q p t", t=PACK)
+            src = y_banks[c, a][:].rearrange("q (t p) -> q p t", t=PACK)
+            if engine == "vector":
+                nc.vector.tensor_copy(out=dst, in_=src)
+            else:
+                nc.scalar.copy(out=dst, in_=src)
+            row = CH * c + P * a
+            nc.sync.dma_start(out=out_0[row : row + P, :], in_=y_rows[c, a][:])
+
+        def group_y(c, copy):
+            y_grouped[c] = ring("bf_stage", 4, [P, PACK * CH], BF16)
+            copy(
+                out=y_grouped[c][:].rearrange("p (n t) -> p n t", t=PACK),
+                in_=y_zones[c][:].rearrange("p t n -> p n t"),
+            )
+
+        def quantize_y(c):
+            cols = slice(CH * c, CH * (c + 1))
+            nc.vector.quantize_mx(out=y_codes[:, cols].bitcast(FP8X4), scales=y_scales[:, cols], in_=y_grouped[c][:])
+            nc.sync.dma_start(
+                out=out_1[0, :, cols, :].rearrange("p m t -> p (m t)").bitcast(I32), in_=y_codes[:, cols].bitcast(I32)
+            )
+
+        def store_y_scales(cols):
+            for q in range(4):
+                nc.sync.dma_start(
+                    out=out_2[0, 4 * q : 4 * q + 4, cols].bitcast(I32), in_=y_scales[32 * q : 32 * q + 4, cols].bitcast(I32)
+                )
+
+        tile_banks, tile_th, tile_grouped, tile_f, tile_y = {}, {}, {}, {}, {}
+
+        def correlate_tile(c, h, a):
+            tile_banks[a] = bank()
+            toks = slice(P * a, P * (a + 1))
+            for t in range(PACK):
+                cols = slice(P * t, P * (t + 1))
+                for g in range(3):
+                    if g < 2:
+                        lhsT = dp_codes[h][:, g, 2 * P * t : 2 * P * (t + 1)].bitcast(FP4X4)
+                        lhsT_scale = dp_scales[h][:, g, cols]
+                    else:
+                        lhsT = da_codes[h][:, cols].bitcast(FP8X4)
+                        lhsT_scale = da_scales[h][:, cols]
+                    nc.tensor.matmul_mx(
+                        out=tile_banks[a][:, cols], lhsT=lhsT, lhsT_scale=lhsT_scale,
+                        rhs=z_codes[c, g][:, toks].bitcast(FP8X4), rhs_scale=z_scales[c, g][:, toks],
+                        start=(g == 0), stop=(g == 2),
+                    )
+
+        def squash_tile(a):
+            tile_th[a] = ring("tile_th", 2, [P, P * PACK], F32)
+            nc.scalar.activation(
+                out=tile_th[a][:].rearrange("p (n t) -> p n t", t=PACK),
+                in_=tile_banks[a][:].rearrange("p (t n) -> p n t", t=PACK), func=ACT.Tanh,
+            )
+
+        def weigh_tile(h, a):
+            tile_grouped[a] = ring("tile_grouped", 2, [P, P * PACK], BF16)
+            nc.vector.tensor_tensor(
+                out=tile_grouped[a][:].rearrange("p (n t) -> p n t", t=PACK),
+                in0=tile_th[a][:].rearrange("p (n t) -> p n t", t=PACK),
+                in1=cw[:, h, :].unsqueeze(1).to_broadcast([P, P, PACK]),
+                op=ALU.mult,
+            )
+
+        def quantize_h_tile(c, h, a):
+            if a == 0:
+                h_codes[c, h] = ring("h_codes", 4, [P, CH], U32)
+                h_scales[c, h] = ring("h_scales", 4, [P, CH], U8)
+            toks = slice(P * a, P * (a + 1))
+            nc.vector.quantize_mx(
+                out=h_codes[c, h][:, toks].bitcast(FP8X4), scales=h_scales[c, h][:, toks], in_=tile_grouped[a][:]
+            )
+
+        def fuse_tile(c, a):
+            tile_f[a] = bank()
+            toks = slice(P * a, P * (a + 1))
+            for t in range(PACK):
+                cols = slice(P * t, P * (t + 1))
+                for h in range(2):
+                    nc.tensor.matmul_mx(
+                        out=tile_f[a][:, cols], lhsT=w_codes[:, h, cols].bitcast(FP8X4), lhsT_scale=w_scales[:, h, cols],
+                        rhs=h_codes[c, h][:, toks].bitcast(FP8X4), rhs_scale=h_scales[c, h][:, toks],
+                        start=(h == 0), stop=(h == 1),
+                    )
+
+        def join_tile(c, a):
+            if a == 0:
+                y_zones[c] = ring("y_zones", 2, [P, PACK, CH], F32)
+            toks = slice(P * a, P * (a + 1))
+            for t in range(PACK):
+                nc.vector.scalar_tensor_tensor(
+                    out=y_zones[c][:, t, toks], in0=tile_f[a][:, P * t : P * (t + 1)], scalar=vec["gain"][:, t : t + 1],
+                    in1=faded[c][:, t, toks], op0=ALU.mult, op1=ALU.add,
+                )
+
+        def group_y_tile(c, a, copy):
+            tile_y[a] = ring("tile_y", 2, [P, P * PACK], BF16)
+            copy(
+                out=tile_y[a][:].rearrange("p (n t) -> p n t", t=PACK),
+                in_=y_zones[c][:, :, P * a : P * (a + 1)].rearrange("p t n -> p n t"),
+            )
+
+        def quantize_y_tile(c, a):
+            cols = slice(CH * c + P * a, CH * c + P * (a + 1))
+            nc.vector.quantize_mx(out=y_codes[:, cols].bitcast(FP8X4), scales=y_scales[:, cols], in_=tile_y[a][:])
+
+        def store_y_codes(cols):
+            nc.sync.dma_start(
+                out=out_1[0, :, cols, :].rearrange("p m t -> p (m t)").bitcast(I32), in_=y_codes[:, cols].bitcast(I32)
+            )
+
+        order_scales(0)
+        turn_z(0, 0)
+        copy_z(0, 0, 0)
+        copy_z(0, 0, 1)
+        order_dp(0)
+        turn_z(0, 1)
+        copy_z(0, 1, 0)
+        copy_z(0, 1, 1)
+        quantize_z(0, 0)
+        order_scales(1)
+        turn_z(0, 2)
+        copy_z(0, 2, 0)
+        copy_z(0, 2, 1)
+        quantize_z(0, 1)
+        group_da(0, nc.vector.tensor_copy)
+        group_da(1, nc.scalar.copy)
+        quantize_z(0, 2)
+        quantize_da(0)
+        for g in range(3):
+            for t in range(PACK):
+                correlate_pass(0, 0, t, g)
+        order_dp(1)
+        for t in range(PACK):
+            squash(0, 0, t)
+        turn_z(1, 0)
+        copy_z(1, 0, 0)
+        copy_z(1, 0, 1)
+        quantize_da(1)
+        correlate(0, 1)
+        weigh(0, 0)
+        quantize_z(1, 0)
+        quantize_h(0, 0)
+        for t in range(PACK):
+            squash(0, 1, t)
+        turn_z(1, 1)
+        turn_z(1, 2)
+        for g in range(1, 3):
+            copy_z(1, g, 0)
+            copy_z(1, g, 1)
+        order_w()
+        quantize_z(1, 1)
+        quantize_z(1, 2)
+        order_w_scales()
+        turn_prev(0)
+        nc.scalar.copy(out=fade32[:], in_=vec["fade"][:])
+        for t in range(PACK):
+            fade_prev(0, t)
+
+        for c in range(1, NCH):
+            last = c == NCH - 1
+            correlate(c, 0)
+            for t in range(PACK):
+                if c >= 2:
+                    copy_y(c - 2, t, "scalar")
+                squash(c, 0, t)
+            weigh(c - 1, 1)
+            if c >= 2:
+                quantize_y(c - 2)
+            quantize_h(c - 1, 1)
+            if not last:
+                turn_z(c + 1, 0)
+                turn_z(c + 1, 1)
+                for g in range(2):
+                    copy_z(c + 1, g, 0)
+                    copy_z(c + 1, g, 1)
+                fuse(c - 1)
+                weigh(c, 0)
+                for t in range(PACK):
+                    join(c - 1, t)
+                quantize_h(c, 0)
+                quantize_z(c + 1, 0)
+                quantize_z(c + 1, 1)
+                turn_z(c + 1, 2)
+                turn_prev(c)
+                copy_z(c + 1, 2, 0)
+                copy_z(c + 1, 2, 1)
+                group_y(c - 1, nc.vector.tensor_copy)
+                quantize_z(c + 1, 2)
+                correlate(c, 1)
+                fade_prev(c, 0)
+                fade_prev(c, 1)
+                squash(c, 1, 0)
+                fade_prev(c, 2)
+                squash(c, 1, 1)
+                fade_prev(c, 3)
+                squash(c, 1, 2)
+                squash(c, 1, 3)
+                turn_y(c - 1)
+
+        c = NCH - 1
+        turn_prev(c)
+        fuse(c - 1)
+        for t in range(PACK):
+            fade_prev(c, t)
+        for t in range(PACK):
+            join(c - 1, t)
+        correlate_tile(c, 1, 0)
+        squash_tile(0)
+        weigh(c, 0)
+        correlate_tile(c, 1, 1)
+        squash_tile(1)
+        turn_y(c - 1)
+        weigh_tile(1, 0)
+        quantize_h(c, 0)
+        quantize_h_tile(c, 1, 0)
+        weigh_tile(1, 1)
+        correlate_tile(c, 1, 2)
+        copy_y(c - 1, 0, "scalar")
+        copy_y(c - 1, 1, "scalar")
+        squash_tile(2)
+        fuse_tile(c, 0)
+        quantize_h_tile(c, 1, 1)
+        correlate_tile(c, 1, 3)
+        copy_y(c - 1, 2, "scalar")
+        squash_tile(3)
+        copy_y(c - 1, 3, "scalar")
+        weigh_tile(1, 2)
+        join_tile(c, 0)
+        quantize_h_tile(c, 1, 2)
+        fuse_tile(c, 1)
+        weigh_tile(1, 3)
+        fuse_tile(c, 2)
+        join_tile(c, 1)
+        quantize_h_tile(c, 1, 3)
+        turn_y_tile(c, 0)
+        group_y(c - 1, nc.scalar.copy)
+        join_tile(c, 2)
+        fuse_tile(c, 3)
+        turn_y_tile(c, 1)
+        group_y_tile(c, 0, nc.vector.tensor_copy)
+        join_tile(c, 3)
+        copy_y(c, 0, "scalar")
+        turn_y_tile(c, 2)
+        turn_y_tile(c, 3)
+        group_y_tile(c, 1, nc.vector.tensor_copy)
+        quantize_y(c - 1)
+        copy_y(c, 1, "scalar")
+        quantize_y_tile(c, 0)
+        copy_y(c, 2, "scalar")
+        group_y_tile(c, 2, nc.vector.tensor_copy)
+        quantize_y_tile(c, 1)
+        group_y_tile(c, 3, nc.vector.tensor_copy)
+        copy_y(c, 3, "scalar")
+        quantize_y_tile(c, 2)
+        quantize_y_tile(c, 3)
+        store_y_codes(slice(CH * c, T))
+        store_y_scales(slice(0, T))

@@ -57,6 +57,8 @@ def tile_multistatic_range_fusion_k6_kernel(
         warm = held("warm", [P, 8], F32)
         nc.vector.memset(warm[:], 0.0)
         warm_out = held("warm_out", [P, 8], F32)
+        zeros = held("zeros", [P, CH], BF16)
+        nc.gpsimd.memset(zeros[:], 0.0)
         ident = held("ident", [P, P], F32)
         make_identity(nc, ident[:])
 
@@ -77,7 +79,7 @@ def tile_multistatic_range_fusion_k6_kernel(
             )
 
         def load_da(h):
-            da_raw[h] = held("da_raw%d" % h, [P, PACK, KPASS], BF16)
+            da_raw[h] = ring("z_pre", 4, [P, PACK, KPASS], BF16)
             nc.sync.dma_start(
                 out=da_raw[h][:], in_=da[:, KPASS * h : KPASS * (h + 1)].rearrange("(p j) c -> p j c", j=PACK)
             )
@@ -91,18 +93,21 @@ def tile_multistatic_range_fusion_k6_kernel(
                 nc.sync.dma_start(out=z_raw[c, g][:, a : a + step, :], in_=rows[:, a : a + step, :])
 
         def load_prev(c):
-            prev_raw[c] = held("prev_raw%d" % c, [P, TT, N], BF16)
+            prev_raw[c] = held("prev_raw0" if c == 0 else "z_raw0_%d" % (c - 1), [P, TT, N], BF16)
             nc.sync.dma_start(
                 out=prev_raw[c][:], in_=prev[CH * c : CH * (c + 1), :].rearrange("(a p) k -> p a k", p=P)
             )
 
-        cw = held("cw", [P, 2, PACK], BF16)
-        nc.gpsimd.dma_start(out=cw[:], in_=cell_weight.rearrange("(h p t) -> p h t", h=2, t=PACK))
+        def load_vector(name, src, groups):
+            vec[name] = held(name, [P, groups, PACK], BF16)
+            nc.sync.dma_start(out=vec[name][:], in_=src.rearrange("(h p t) -> p h t", h=groups, t=PACK))
+
         vec = {}
-        for name, src in (("fade", fade), ("bias", bias), ("gain", zone_gain)):
-            vec[name] = held(name, [P, PACK], BF16)
-            nc.gpsimd.dma_start(out=vec[name][:], in_=src.rearrange("(p t) -> p t", t=PACK))
         fade32 = held("fade32", [P, PACK], F32)
+
+        def cast_fade():
+            nc.scalar.copy(out=fade32[:], in_=vec["fade"][:, 0, :])
+
 
         load_z(0, 0)
         load_dp(0)
@@ -111,9 +116,14 @@ def tile_multistatic_range_fusion_k6_kernel(
         load_da(0)
         load_dp(1)
         load_da(1)
+        load_vector("cw", cell_weight, 2)
         for g in range(3):
             load_z(1, g)
+        load_vector("fade", fade, 1)
+        load_vector("bias", bias, 1)
         load_prev(0)
+        load_vector("gain", zone_gain, 1)
+        cw = vec["cw"]
         w_raw = held("w_raw", [P, 2, N], U32)
         nc.sync.dma_start(out=w_raw[:].bitcast(I32), in_=fuse_words.rearrange("g p n t -> p g (n t)").bitcast(I32))
         for q in range(4):
@@ -146,10 +156,16 @@ def tile_multistatic_range_fusion_k6_kernel(
 
         def group_da(h, copy):
             da_grouped[h] = ring("h_grouped", 2, [P, PACK * CH], BF16)
-            copy(
-                out=da_grouped[h][:].rearrange("p (t m j) -> p t m j", t=PACK, j=PACK),
-                in_=da_raw[h][:].rearrange("p j (m t) -> p t m j", t=PACK),
-            )
+            if h == 0:
+                copy(
+                    out=da_grouped[h][:].rearrange("p (t m i j) -> p m t i j", t=PACK, i=2, j=PACK),
+                    in_=da_raw[h][:].rearrange("p j (m i t) -> p m t i j", t=PACK, i=2),
+                )
+            else:
+                copy(
+                    out=da_grouped[h][:].rearrange("p (t m j) -> p t m j", t=PACK, j=PACK),
+                    in_=da_raw[h][:].rearrange("p j (m t) -> p t m j", t=PACK),
+                )
 
         def quantize_da(h):
             da_codes[h] = held("da_codes%d" % h, [P, KPASS], U32)
@@ -168,30 +184,43 @@ def tile_multistatic_range_fusion_k6_kernel(
 
         def order_w():
             nc.vector.tensor_copy(
-                out=w_codes[:].bitcast(I32).rearrange("p g (t m) -> p g t m", t=PACK),
-                in_=w_raw[:].bitcast(I32).rearrange("p g (m t) -> p g t m", t=PACK),
+                out=w_codes[:].bitcast(I32).rearrange("p g (t m i) -> p g m t i", t=PACK, i=2),
+                in_=w_raw[:].bitcast(I32).rearrange("p g (m i t) -> p g m t i", t=PACK, i=2),
             )
 
-        z_banks, z_grouped, z_codes, z_scales = {}, {}, {}, {}
+        def warm_up(count):
+            idle = bank()
+            for i in range(count):
+                nc.tensor.matmul(idle[:], lhsT=zeros[:, :P], rhs=zeros[:], start=True, stop=True)
 
-        def turn_z(c, g):
-            words = z_raw[c, g][:].bitcast(F32)
-            for half in range(2):
-                z_banks[c, g, half] = bank()
-                for a in range(2):
-                    for u in range(2):
-                        col = 2 * P * u + P * a
-                        nc.tensor.transpose(
-                            z_banks[c, g, half][:, col : col + P], words[:, 2 * half + a, u :: 2], ident[:]
-                        )
+        z_banks, z_grouped, z_codes, z_scales, z_pre, prev_pre = {}, {}, {}, {}, {}, {}
+
+        def order_words(raw, copy):
+            ordered = ring("z_pre", 4, [P, 2, TT * P], F32)
+            copy(
+                out=ordered[:].rearrange("p u (m i) -> p m u i", i=2),
+                in_=raw[:].bitcast(F32).rearrange("p a (m i u) -> p (a m) u i", i=2, u=2),
+            )
+            return ordered
+
+        def order_z(c, g, copy):
+            z_pre[c, g] = order_words(z_raw[c, g], copy)
+
+        def z_words(c, g, a, u):
+            if (c, g) in z_pre:
+                return z_pre[c, g][:, u, P * a : P * (a + 1)]
+            return z_raw[c, g][:].bitcast(F32)[:, a, u::2]
 
         def turn_z_half(c, g, half):
-            words = z_raw[c, g][:].bitcast(F32)
             z_banks[c, g, half] = bank()
             for a in range(2):
                 for u in range(2):
                     col = 2 * P * u + P * a
-                    nc.tensor.transpose(z_banks[c, g, half][:, col : col + P], words[:, 2 * half + a, u :: 2], ident[:])
+                    nc.tensor.transpose(z_banks[c, g, half][:, col : col + P], z_words(c, g, 2 * half + a, u), ident[:])
+
+        def turn_z(c, g):
+            for half in range(2):
+                turn_z_half(c, g, half)
 
         def copy_z(c, g, half):
             if half == 0:
@@ -246,9 +275,9 @@ def tile_multistatic_range_fusion_k6_kernel(
         def weigh(c, h):
             h_grouped[c, h] = ring("h_grouped", 2, [P, PACK * CH], BF16)
             nc.vector.tensor_tensor(
-                out=h_grouped[c, h][:].rearrange("p (n t) -> p n t", t=PACK),
-                in0=th[c, h][:].rearrange("p t n -> p n t"),
-                in1=cw[:, h, :].unsqueeze(1).to_broadcast([P, CH, PACK]),
+                out=h_grouped[c, h][:].rearrange("p (n i t) -> p n t i", i=2, t=PACK),
+                in0=th[c, h][:].rearrange("p t (n i) -> p n t i", i=2),
+                in1=cw[:, h, :].unsqueeze(1).unsqueeze(3).to_broadcast([P, CH // 2, PACK, 2]),
                 op=ALU.mult,
             )
 
@@ -259,18 +288,18 @@ def tile_multistatic_range_fusion_k6_kernel(
 
         prev_banks, faded, f_banks, y_zones = {}, {}, {}, {}
 
-        def turn_prev(c):
-            words = prev_raw[c][:].bitcast(F32)
-            for u in range(2):
-                prev_banks[c, u] = bank()
-                for a in range(TT):
-                    nc.tensor.transpose(prev_banks[c, u][:, P * a : P * (a + 1)], words[:, a, u :: 2], ident[:])
+        def order_prev(c, copy):
+            prev_pre[c] = order_words(prev_raw[c], copy)
 
         def turn_prev_half(c, u):
-            words = prev_raw[c][:].bitcast(F32)
             prev_banks[c, u] = bank()
             for a in range(TT):
-                nc.tensor.transpose(prev_banks[c, u][:, P * a : P * (a + 1)], words[:, a, u :: 2], ident[:])
+                words = prev_pre[c][:, u, P * a : P * (a + 1)] if c in prev_pre else prev_raw[c][:].bitcast(F32)[:, a, u::2]
+                nc.tensor.transpose(prev_banks[c, u][:, P * a : P * (a + 1)], words, ident[:])
+
+        def turn_prev(c):
+            for u in range(2):
+                turn_prev_half(c, u)
 
         def fade_prev(c, t):
             if t == 0:
@@ -278,7 +307,7 @@ def tile_multistatic_range_fusion_k6_kernel(
             pair = prev_banks[c, t // 2][:].bitcast(BF16).rearrange("p (n e) -> p e n", e=2)
             nc.scalar.activation(
                 out=faded[c][:, t, :], in_=pair[:, t % 2, :], func=ACT.Identity,
-                scale=fade32[:, t : t + 1], bias=vec["bias"][:, t : t + 1],
+                scale=fade32[:, t : t + 1], bias=vec["bias"][:, 0, t : t + 1],
             )
 
         def fuse_pass(c, t, h):
@@ -304,7 +333,7 @@ def tile_multistatic_range_fusion_k6_kernel(
             if t == 0:
                 y_zones[c] = ring("y_zones", 2, [P, PACK, CH], F32)
             nc.vector.scalar_tensor_tensor(
-                out=y_zones[c][:, t, :], in0=f_banks[c, t][:], scalar=vec["gain"][:, t : t + 1],
+                out=y_zones[c][:, t, :], in0=f_banks[c, t][:], scalar=vec["gain"][:, 0, t : t + 1],
                 in1=faded[c][:, t, :], op0=ALU.mult, op1=ALU.add,
             )
 
@@ -337,8 +366,8 @@ def tile_multistatic_range_fusion_k6_kernel(
         def group_y(c, copy):
             y_grouped[c] = ring("bf_stage", 4, [P, PACK * CH], BF16)
             copy(
-                out=y_grouped[c][:].rearrange("p (n t) -> p n t", t=PACK),
-                in_=y_zones[c][:].rearrange("p t n -> p n t"),
+                out=y_grouped[c][:].rearrange("p (n i t) -> p n t i", i=2, t=PACK),
+                in_=y_zones[c][:].rearrange("p t (n i) -> p n t i", i=2),
             )
 
         def quantize_y(c):
@@ -417,15 +446,15 @@ def tile_multistatic_range_fusion_k6_kernel(
             toks = slice(P * a, P * (a + 1))
             for t in range(PACK):
                 nc.vector.scalar_tensor_tensor(
-                    out=y_zones[c][:, t, toks], in0=tile_f[a][:, P * t : P * (t + 1)], scalar=vec["gain"][:, t : t + 1],
+                    out=y_zones[c][:, t, toks], in0=tile_f[a][:, P * t : P * (t + 1)], scalar=vec["gain"][:, 0, t : t + 1],
                     in1=faded[c][:, t, toks], op0=ALU.mult, op1=ALU.add,
                 )
 
         def group_y_tile(c, a, copy):
             tile_y[a] = ring("tile_y", 2, [P, P * PACK], BF16)
             copy(
-                out=tile_y[a][:].rearrange("p (n t) -> p n t", t=PACK),
-                in_=y_zones[c][:, :, P * a : P * (a + 1)].rearrange("p t n -> p n t"),
+                out=tile_y[a][:].rearrange("p (n i t) -> p n t i", i=2, t=PACK),
+                in_=y_zones[c][:, :, P * a : P * (a + 1)].rearrange("p t (n i) -> p n t i", i=2),
             )
 
         def quantize_y_tile(c, a):
@@ -438,149 +467,232 @@ def tile_multistatic_range_fusion_k6_kernel(
             )
 
         order_scales(0)
-        turn_z(0, 0)
+        warm_up(7)
+        turn_z_half(0, 0, 0)
+        turn_z_half(0, 0, 1)
+        warm_up(2)
+        order_dp(0)
+        turn_z_half(0, 1, 0)
+        order_scales(1)
         copy_z(0, 0, 0)
         copy_z(0, 0, 1)
-        order_dp(0)
-        turn_z(0, 1)
+        turn_z_half(0, 1, 1)
         copy_z(0, 1, 0)
-        copy_z(0, 1, 1)
         quantize_z(0, 0)
-        order_scales(1)
-        turn_z(0, 2)
+        turn_z_half(0, 2, 0)
+        copy_z(0, 1, 1)
+        turn_z_half(0, 2, 1)
         copy_z(0, 2, 0)
-        copy_z(0, 2, 1)
         quantize_z(0, 1)
+        correlate_pass(0, 0, 0, 0)
         group_da(0, nc.vector.tensor_copy)
-        group_da(1, nc.scalar.copy)
+        copy_z(0, 2, 1)
         quantize_z(0, 2)
+        correlate_pass(0, 0, 1, 0)
         quantize_da(0)
-        for g in range(3):
-            for t in range(PACK):
-                correlate_pass(0, 0, t, g)
+        correlate_pass(0, 0, 0, 1)
+        group_da(1, nc.scalar.copy)
+        correlate_pass(0, 0, 1, 1)
         order_dp(1)
-        for t in range(PACK):
-            squash(0, 0, t)
-        turn_z(1, 0)
+        order_z(1, 1, nc.vector.tensor_copy)
+        correlate_pass(0, 0, 2, 0)
+        correlate_pass(0, 0, 3, 0)
+        correlate_pass(0, 0, 2, 1)
+        correlate_pass(0, 0, 3, 1)
+        correlate_pass(0, 0, 0, 2)
+        correlate_pass(0, 0, 1, 2)
+        squash(0, 0, 0)
+        quantize_da(1)
+        correlate_pass(0, 0, 2, 2)
+        correlate_pass(0, 0, 3, 2)
+        turn_z_half(1, 0, 0)
+        order_z(1, 2, nc.vector.tensor_copy)
+        turn_z_half(1, 0, 1)
+        squash(0, 0, 1)
+        correlate_group(0, 1, 0)
+        squash(0, 0, 2)
+        squash(0, 0, 3)
+        correlate_group(0, 1, 1)
+        turn_z_half(1, 2, 0)
+        turn_z_half(1, 1, 0)
+        weigh(0, 0)
         copy_z(1, 0, 0)
         copy_z(1, 0, 1)
-        quantize_da(1)
-        correlate(0, 1)
-        weigh(0, 0)
-        quantize_z(1, 0)
-        quantize_h(0, 0)
-        for t in range(PACK):
-            squash(0, 1, t)
-        turn_z(1, 1)
-        turn_z(1, 2)
-        for g in range(1, 3):
-            copy_z(1, g, 0)
-            copy_z(1, g, 1)
-        order_w()
-        quantize_z(1, 1)
-        quantize_z(1, 2)
+        squash(0, 1, 0)
+        squash(0, 1, 1)
+        turn_z_half(1, 1, 1)
+        copy_z(1, 2, 0)
+        cast_fade()
+        copy_z(1, 1, 0)
+        copy_z(1, 1, 1)
+        correlate_group(0, 1, 2)
         order_w_scales()
-        turn_prev(0)
-        nc.scalar.copy(out=fade32[:], in_=vec["fade"][:])
-        for t in range(PACK):
-            fade_prev(0, t)
-
-        for c in range(1, NCH):
-            last = c == NCH - 1
-            correlate(c, 0)
-            for t in range(PACK):
-                if c >= 2:
-                    copy_y(c - 2, t, "scalar")
-                squash(c, 0, t)
+        quantize_h(0, 0)
+        quantize_z(1, 0)
+        turn_z_half(1, 2, 1)
+        turn_prev_half(0, 0)
+        copy_z(1, 2, 1)
+        quantize_z(1, 1)
+        fade_prev(0, 0)
+        squash(0, 1, 2)
+        quantize_z(1, 2)
+        turn_prev_half(0, 1)
+        correlate_group(0, 1, 3)
+        squash(0, 1, 3)
+        fade_prev(0, 1)
+        order_w()
+        fade_prev(0, 2)
+        fade_prev(0, 3)
+        for c in (1, 2):
+            order_z(c + 1, 0, nc.vector.tensor_copy)
+            if c >= 2:
+                copy_y(c - 2, 0, 'scalar')
+            if c >= 2:
+                copy_y(c - 2, 1, 'scalar')
+            correlate_group(c, 0, 0)
+            correlate_group(c, 0, 1)
+            if c >= 2:
+                copy_y(c - 2, 2, 'scalar')
+            correlate_group(c, 0, 2)
+            correlate_group(c, 0, 3)
+            turn_z_half(c + 1, 0, 0)
             weigh(c - 1, 1)
+            squash(c, 0, 0)
+            turn_z_half(c + 1, 0, 1)
+            squash(c, 0, 1)
+            order_z(c + 1, 1, nc.vector.tensor_copy)
+            turn_z_half(c + 1, 1, 0)
+            quantize_h(c - 1, 1)
+            if c >= 2:
+                copy_y(c - 2, 3, 'scalar')
+            order_z(c + 1, 2, nc.vector.tensor_copy)
+            squash(c, 0, 2)
+            turn_z_half(c + 1, 1, 1)
+            fuse_group(c - 1, 0)
+            squash(c, 0, 3)
+            copy_z(c + 1, 0, 0)
+            fuse_group(c - 1, 1)
+            copy_z(c + 1, 0, 1)
+            fuse_group(c - 1, 2)
+            fuse_group(c - 1, 3)
+            copy_z(c + 1, 1, 0)
+            order_prev(c, nc.scalar.copy)
+            turn_z_half(c + 1, 2, 0)
+            weigh(c, 0)
+            join(c - 1, 0)
+            turn_z_half(c + 1, 2, 1)
+            join(c - 1, 1)
+            copy_z(c + 1, 1, 1)
+            turn_prev_half(c, 0)
+            join(c - 1, 2)
+            copy_z(c + 1, 2, 0)
+            turn_prev_half(c, 1)
+            correlate_group(c, 1, 0)
+            correlate_group(c, 1, 1)
+            copy_z(c + 1, 2, 1)
+            quantize_z(c + 1, 0)
+            join(c - 1, 3)
+            quantize_z(c + 1, 1)
+            correlate_group(c, 1, 2)
+            correlate_group(c, 1, 3)
+            fade_prev(c, 0)
+            squash(c, 1, 0)
             if c >= 2:
                 quantize_y(c - 2)
-            quantize_h(c - 1, 1)
-            if not last:
-                turn_z(c + 1, 0)
-                turn_z(c + 1, 1)
-                for g in range(2):
-                    copy_z(c + 1, g, 0)
-                    copy_z(c + 1, g, 1)
-                fuse(c - 1)
-                weigh(c, 0)
-                for t in range(PACK):
-                    join(c - 1, t)
-                quantize_h(c, 0)
-                quantize_z(c + 1, 0)
-                quantize_z(c + 1, 1)
-                turn_z(c + 1, 2)
-                turn_prev(c)
-                copy_z(c + 1, 2, 0)
-                copy_z(c + 1, 2, 1)
-                group_y(c - 1, nc.vector.tensor_copy)
-                quantize_z(c + 1, 2)
-                correlate(c, 1)
-                fade_prev(c, 0)
-                fade_prev(c, 1)
-                squash(c, 1, 0)
-                fade_prev(c, 2)
-                squash(c, 1, 1)
-                fade_prev(c, 3)
-                squash(c, 1, 2)
-                squash(c, 1, 3)
-                turn_y(c - 1)
-
-        c = NCH - 1
-        turn_prev(c)
-        fuse(c - 1)
-        for t in range(PACK):
-            fade_prev(c, t)
-        for t in range(PACK):
-            join(c - 1, t)
-        correlate_tile(c, 1, 0)
+            quantize_z(c + 1, 2)
+            fade_prev(c, 1)
+            group_y(c - 1, nc.vector.tensor_copy)
+            turn_y_tile(c - 1, 0)
+            turn_y_tile(c - 1, 1)
+            fade_prev(c, 2)
+            fade_prev(c, 3)
+            squash(c, 1, 1)
+            turn_y_tile(c - 1, 2)
+            turn_y_tile(c - 1, 3)
+            squash(c, 1, 2)
+            squash(c, 1, 3)
+            quantize_h(c, 0)
+        copy_y(1, 0, 'scalar')
+        correlate_group(3, 0, 0)
+        copy_y(1, 1, 'scalar')
+        order_prev(3, nc.vector.tensor_copy)
+        correlate_group(3, 0, 1)
+        copy_y(1, 2, 'scalar')
+        correlate_group(3, 0, 2)
+        weigh(2, 1)
+        copy_y(1, 3, 'scalar')
+        turn_prev_half(3, 0)
+        squash(3, 0, 0)
+        squash(3, 0, 1)
+        fade_prev(3, 0)
+        squash(3, 0, 2)
+        turn_prev_half(3, 1)
+        quantize_h(2, 1)
+        correlate_group(3, 0, 3)
+        fuse_group(2, 0)
+        fuse_group(2, 1)
+        fuse_group(2, 2)
+        quantize_y(1)
+        join(2, 0)
+        fuse_group(2, 3)
+        join(2, 1)
+        fade_prev(3, 1)
+        correlate_tile(3, 1, 0)
+        join(2, 2)
+        fade_prev(3, 2)
+        join(2, 3)
+        correlate_tile(3, 1, 1)
+        fade_prev(3, 3)
+        turn_y_tile(2, 0)
+        squash(3, 0, 3)
         squash_tile(0)
-        weigh(c, 0)
-        correlate_tile(c, 1, 1)
+        weigh(3, 0)
+        turn_y_tile(2, 1)
         squash_tile(1)
-        turn_y(c - 1)
+        turn_y_tile(2, 2)
         weigh_tile(1, 0)
-        quantize_h(c, 0)
-        quantize_h_tile(c, 1, 0)
-        weigh_tile(1, 1)
-        correlate_tile(c, 1, 2)
-        copy_y(c - 1, 0, "scalar")
-        copy_y(c - 1, 1, "scalar")
+        copy_y(2, 0, 'scalar')
+        copy_y(2, 1, 'scalar')
+        quantize_h(3, 0)
+        turn_y_tile(2, 3)
+        copy_y(2, 2, 'scalar')
+        correlate_tile(3, 1, 2)
         squash_tile(2)
-        fuse_tile(c, 0)
-        quantize_h_tile(c, 1, 1)
-        correlate_tile(c, 1, 3)
-        copy_y(c - 1, 2, "scalar")
-        squash_tile(3)
-        copy_y(c - 1, 3, "scalar")
+        copy_y(2, 3, 'scalar')
+        weigh_tile(1, 1)
+        quantize_h_tile(3, 1, 0)
+        correlate_tile(3, 1, 3)
+        fuse_tile(3, 0)
+        quantize_h_tile(3, 1, 1)
         weigh_tile(1, 2)
-        join_tile(c, 0)
-        quantize_h_tile(c, 1, 2)
-        fuse_tile(c, 1)
+        squash_tile(3)
+        join_tile(3, 0)
+        quantize_h_tile(3, 1, 2)
+        fuse_tile(3, 1)
+        group_y(2, nc.scalar.copy)
+        join_tile(3, 1)
         weigh_tile(1, 3)
-        fuse_tile(c, 2)
-        join_tile(c, 1)
-        quantize_h_tile(c, 1, 3)
-        turn_y_tile(c, 0)
-        group_y(c - 1, nc.scalar.copy)
-        join_tile(c, 2)
-        fuse_tile(c, 3)
-        turn_y_tile(c, 1)
-        group_y_tile(c, 0, nc.vector.tensor_copy)
-        join_tile(c, 3)
-        copy_y(c, 0, "scalar")
-        turn_y_tile(c, 2)
-        turn_y_tile(c, 3)
-        group_y_tile(c, 1, nc.vector.tensor_copy)
-        quantize_y(c - 1)
-        copy_y(c, 1, "scalar")
-        quantize_y_tile(c, 0)
-        copy_y(c, 2, "scalar")
-        group_y_tile(c, 2, nc.vector.tensor_copy)
-        quantize_y_tile(c, 1)
-        group_y_tile(c, 3, nc.vector.tensor_copy)
-        copy_y(c, 3, "scalar")
-        quantize_y_tile(c, 2)
-        quantize_y_tile(c, 3)
-        store_y_codes(slice(CH * c, T))
-        store_y_scales(slice(0, T))
+        turn_y_tile(3, 0)
+        fuse_tile(3, 2)
+        group_y_tile(3, 0, nc.vector.tensor_copy)
+        turn_y_tile(3, 1)
+        copy_y(3, 0, 'scalar')
+        copy_y(3, 1, 'scalar')
+        quantize_h_tile(3, 1, 3)
+        join_tile(3, 2)
+        quantize_y(2)
+        fuse_tile(3, 3)
+        join_tile(3, 3)
+        turn_y_tile(3, 2)
+        group_y_tile(3, 1, nc.vector.tensor_copy)
+        turn_y_tile(3, 3)
+        copy_y(3, 2, 'scalar')
+        quantize_y_tile(3, 0)
+        group_y_tile(3, 2, nc.vector.tensor_copy)
+        quantize_y_tile(3, 1)
+        group_y_tile(3, 3, nc.vector.tensor_copy)
+        quantize_y_tile(3, 2)
+        quantize_y_tile(3, 3)
+        copy_y(3, 3, 'scalar')
+        store_y_codes(slice(1536, 2048))
+        store_y_scales(slice(0, 2048))

@@ -20,9 +20,12 @@ P = 128
 PACK = 4
 KPASS = P * PACK
 CH = 512
-NCH = T // CH
-TT = CH // P
+HALF = CH // 2
+LAST = T // CH - 1
 BANKS = 8
+ZA = 2
+W_ROW = 4
+WARM_FIRST, WARM_BETWEEN = 7, 2
 
 
 def tile_multistatic_range_fusion_k6_kernel(
@@ -30,114 +33,109 @@ def tile_multistatic_range_fusion_k6_kernel(
     zone_gain, fade, prev, bias, out_0, out_1, out_2,
 ):
     nc = tc.nc
+    on_vector, on_scalar = nc.vector.tensor_copy, nc.scalar.copy
     with ExitStack() as ctx:
-        keep = ctx.enter_context(tc.tile_pool(name="keep", bufs=1))
+        sbuf = ctx.enter_context(tc.tile_pool(name="sbuf", bufs=1))
         psum = ctx.enter_context(tc.psum_pool(name="psum", bufs=1))
         ctx.enter_context(tc.manual_schedule())
 
         turns = {}
 
-        def ring(name, depth, shape, dtype):
-            turn = turns.get(name, 0)
-            turns[name] = turn + 1
-            return keep.tile(shape, dtype, name=name, tag="%s%d" % (name, turn % depth), align_bytes=64)
+        def next_turn(name):
+            turns[name] = turns.get(name, -1) + 1
+            return turns[name]
 
         def held(name, shape, dtype):
-            return keep.tile(shape, dtype, name=name, tag=name, align_bytes=64)
+            return sbuf.tile(shape, dtype, name=name, tag=name, align_bytes=64)
+
+        def ring(name, depth, shape, dtype):
+            return held("%s%d" % (name, next_turn(name) % depth), shape, dtype)
 
         def bank():
-            turn = turns.get("bank", 0)
-            turns["bank"] = turn + 1
-            return psum.tile([P, CH], F32, name="bank", tag="bank%d" % (turn % BANKS))
+            return psum.tile([P, CH], F32, name="bank", tag="bank%d" % (next_turn("bank") % BANKS))
 
         scale_raw = held("scale_raw", [P, 2, G], U8)
         nc.vector.memset(scale_raw[:].rearrange("p g n -> p (g n)").bitcast(I32), 0)
-        w_scale_raw = held("w_scale_raw", [P, 2, N], U8)
-        nc.vector.memset(w_scale_raw[:].rearrange("p g n -> p (g n)").bitcast(I32), 0)
-        warm = held("warm", [P, 8], F32)
-        nc.vector.memset(warm[:], 0.0)
-        warm_out = held("warm_out", [P, 8], F32)
         zeros = held("zeros", [P, CH], BF16)
         nc.gpsimd.memset(zeros[:], 0.0)
         ident = held("ident", [P, P], F32)
         make_identity(nc, ident[:])
 
-        for q in range(4):
-            nc.scalar.dma_start(
-                out=scale_raw[32 * q : 32 * q + 4, :, :].bitcast(I32),
-                in_=passive_scales[:, 4 * q : 4 * q + 4, :].rearrange("g r n -> r g n").bitcast(I32),
-            )
-        nc.scalar.activation(out=warm_out[:], in_=warm[:], func=ACT.Tanh)
+        def load_scale_rows(queue, src, row, cols):
+            for q in range(4):
+                queue.dma_start(
+                    out=scale_raw[32 * q + row : 32 * q + row + 4, :, cols].bitcast(I32),
+                    in_=src[:, 4 * q : 4 * q + 4, :].rearrange("g r n -> r g n").bitcast(I32),
+                )
 
-        dp_raw, da_raw, z_raw, prev_raw = {}, {}, {}, {}
+        load_scale_rows(nc.scalar, passive_scales, 0, slice(0, G))
+        table_warm = held("table_warm", [P, 8], F32)
+        nc.scalar.activation(out=table_warm[:], in_=zeros[:, :8], func=ACT.Tanh)
+
+        dp_raw, da_raw, z_raw, prev_raw, vec = {}, {}, {}, {}, {}
 
         def load_dp(h):
             dp_raw[h] = held("dp_raw%d" % h, [P, 2, 2 * KPASS], U8)
-            nc.sync.dma_start(
-                out=dp_raw[h][:].bitcast(I32),
-                in_=passive_words[:, :, 2 * KPASS * h : 2 * KPASS * (h + 1)].rearrange("g p n -> p g n").bitcast(I32),
-            )
+            src = passive_words[:, :, 2 * KPASS * h : 2 * KPASS * (h + 1)]
+            nc.sync.dma_start(out=dp_raw[h][:].bitcast(I32), in_=src.rearrange("g p n -> p g n").bitcast(I32))
 
         def load_da(h):
-            da_raw[h] = ring("z_pre", 4, [P, PACK, KPASS], BF16)
-            nc.sync.dma_start(
-                out=da_raw[h][:], in_=da[:, KPASS * h : KPASS * (h + 1)].rearrange("(p j) c -> p j c", j=PACK)
-            )
+            da_raw[h] = ring("staged", 4, [P, PACK, KPASS], BF16)
+            src = da[:, KPASS * h : KPASS * (h + 1)]
+            nc.sync.dma_start(out=da_raw[h][:], in_=src.rearrange("(p j) n -> p j n", j=PACK))
 
-        def load_z(c, g, pieces=1):
-            src = zp[:, KPASS * g : KPASS * (g + 1)] if g < 2 else za
-            z_raw[c, g] = held("z_raw%d_%d" % (c, g), [P, TT, KPASS], BF16)
-            rows = src[CH * c : CH * (c + 1), :].rearrange("(a p) k -> p a k", p=P)
-            step = TT // pieces
-            for a in range(0, TT, step):
-                nc.sync.dma_start(out=z_raw[c, g][:, a : a + step, :], in_=rows[:, a : a + step, :])
+        def load_zp(c, half):
+            row = CH * c + HALF * half
+            z_raw[c, half] = held("z_raw%d_%d" % (c, half), [P, 2, KP], BF16)
+            nc.sync.dma_start(out=z_raw[c, half][:], in_=zp[row : row + HALF, :].rearrange("(r j) k -> r j k", j=2))
+
+        def chunk_rows(src, c):
+            return src[CH * c : CH * (c + 1), :].rearrange("(a r j) k -> r a (j k)", a=2, j=2)
+
+        def load_za(c, halves):
+            if (c, ZA) not in z_raw:
+                z_raw[c, ZA] = held("z_raw%d_%d" % (c, ZA), [P, 2, 2 * KA], BF16)
+            nc.sync.dma_start(out=z_raw[c, ZA][:, halves, :], in_=chunk_rows(za, c)[:, halves, :])
 
         def load_prev(c):
-            prev_raw[c] = held("prev_raw0" if c == 0 else "z_raw0_%d" % (c - 1), [P, TT, N], BF16)
-            nc.sync.dma_start(
-                out=prev_raw[c][:], in_=prev[CH * c : CH * (c + 1), :].rearrange("(a p) k -> p a k", p=P)
-            )
+            prev_raw[c] = held("prev_raw" if c == 0 else "z_raw0_%d" % (c - 1), [P, 2, 2 * N], BF16)
+            nc.sync.dma_start(out=prev_raw[c][:], in_=chunk_rows(prev, c))
 
-        def load_vector(name, src, groups):
+        def load_vector(name, src):
+            groups = src.shape[0] // KPASS
             vec[name] = held(name, [P, groups, PACK], BF16)
             nc.sync.dma_start(out=vec[name][:], in_=src.rearrange("(h p t) -> p h t", h=groups, t=PACK))
 
-        vec = {}
-        fade32 = held("fade32", [P, PACK], F32)
-
-        def cast_fade():
-            nc.scalar.copy(out=fade32[:], in_=vec["fade"][:, 0, :])
-
-
-        load_z(0, 0)
-        load_dp(0)
-        load_z(0, 1)
-        load_z(0, 2)
-        load_da(0)
-        load_dp(1)
-        load_da(1)
-        load_vector("cw", cell_weight, 2)
-        for g in range(3):
-            load_z(1, g)
-        load_vector("fade", fade, 1)
-        load_vector("bias", bias, 1)
-        load_prev(0)
-        load_vector("gain", zone_gain, 1)
-        cw = vec["cw"]
         w_raw = held("w_raw", [P, 2, N], U32)
-        nc.sync.dma_start(out=w_raw[:].bitcast(I32), in_=fuse_words.rearrange("g p n t -> p g (n t)").bitcast(I32))
-        for q in range(4):
-            nc.sync.dma_start(
-                out=w_scale_raw[32 * q : 32 * q + 4, :, :].bitcast(I32),
-                in_=fuse_scales[:, 4 * q : 4 * q + 4, :].rearrange("g r n -> r g n").bitcast(I32),
-            )
-        for c in range(2, NCH):
-            for g in range(3):
-                load_z(c, g)
-            load_prev(c - 1)
-        load_prev(NCH - 1)
 
-        dp_codes, dp_scales, da_grouped, da_codes, da_scales = {}, {}, {}, {}, {}
+        load_zp(0, 0)
+        load_dp(0)
+        load_zp(0, 1)
+        load_za(0, slice(0, 1))
+        load_za(0, slice(1, 2))
+        load_da(0)
+        load_da(1)
+        load_vector("bias", bias)
+        load_vector("fade", fade)
+        load_dp(1)
+        load_zp(1, 0)
+        load_scale_rows(nc.sync, fuse_scales, W_ROW, slice(KPASS, G))
+        load_prev(0)
+        load_vector("cell_weight", cell_weight)
+        load_zp(1, 1)
+        load_vector("gain", zone_gain)
+        nc.sync.dma_start(out=w_raw[:].bitcast(I32), in_=fuse_words.rearrange("g p n t -> p g (n t)").bitcast(I32))
+        load_za(1, slice(0, 2))
+        for c in range(2, LAST + 1):
+            load_zp(c, 0)
+            load_zp(c, 1)
+            load_za(c, slice(0, 2))
+            load_prev(c - 1)
+        load_prev(LAST)
+
+        dp_codes, scales, da_grouped, da_codes, da_scales = {}, {}, {}, {}, {}
+        w_codes = held("w_codes", [P, 2, N], U32)
+        fade32 = held("fade32", [P, PACK], F32)
 
         def order_dp(h):
             dp_codes[h] = held("dp_codes%d" % h, [P, 2, 2 * KPASS], U8)
@@ -148,38 +146,10 @@ def tile_multistatic_range_fusion_k6_kernel(
                 )
 
         def order_scales(h):
-            dp_scales[h] = held("dp_scales%d" % h, [P, 2, KPASS], U8)
+            scales[h] = held("scales%d" % h, [P, 2, KPASS], U8)
             nc.vector.tensor_copy(
-                out=dp_scales[h][:].rearrange("p g (t m) -> p g t m", t=PACK),
+                out=scales[h][:].rearrange("p g (t m) -> p g t m", t=PACK),
                 in_=scale_raw[:, :, KPASS * h : KPASS * (h + 1)].rearrange("p g (m t) -> p g t m", t=PACK),
-            )
-
-        def group_da(h, copy):
-            da_grouped[h] = ring("h_grouped", 2, [P, PACK * CH], BF16)
-            if h == 0:
-                copy(
-                    out=da_grouped[h][:].rearrange("p (t m i j) -> p m t i j", t=PACK, i=2, j=PACK),
-                    in_=da_raw[h][:].rearrange("p j (m i t) -> p m t i j", t=PACK, i=2),
-                )
-            else:
-                copy(
-                    out=da_grouped[h][:].rearrange("p (t m j) -> p t m j", t=PACK, j=PACK),
-                    in_=da_raw[h][:].rearrange("p j (m t) -> p t m j", t=PACK),
-                )
-
-        def quantize_da(h):
-            da_codes[h] = held("da_codes%d" % h, [P, KPASS], U32)
-            da_scales[h] = held("da_scales%d" % h, [P, KPASS], U8)
-            nc.vector.quantize_mx(out=da_codes[h][:].bitcast(FP8X4), scales=da_scales[h][:], in_=da_grouped[h][:])
-
-        w_codes = held("w_codes", [P, 2, N], U32)
-
-        w_scales = held("w_scales", [P, 2, N], U8)
-
-        def order_w_scales():
-            nc.vector.tensor_copy(
-                out=w_scales[:].rearrange("p g (t m) -> p g t m", t=PACK),
-                in_=w_scale_raw[:].rearrange("p g (m t) -> p g t m", t=PACK),
             )
 
         def order_w():
@@ -188,511 +158,472 @@ def tile_multistatic_range_fusion_k6_kernel(
                 in_=w_raw[:].bitcast(I32).rearrange("p g (m i t) -> p g m t i", t=PACK, i=2),
             )
 
+        def group_da_on_vector(h):
+            da_grouped[h] = ring("h_grouped", 2, [P, PACK * KPASS], BF16)
+            nc.vector.tensor_copy(
+                out=da_grouped[h][:].rearrange("p (t m i j) -> p m t i j", t=PACK, i=2, j=PACK),
+                in_=da_raw[h][:].rearrange("p j (m i t) -> p m t i j", t=PACK, i=2),
+            )
+
+        def group_da_on_scalar(h):
+            da_grouped[h] = ring("h_grouped", 2, [P, PACK * KPASS], BF16)
+            nc.scalar.copy(
+                out=da_grouped[h][:].rearrange("p (t m j) -> p t m j", t=PACK, j=PACK),
+                in_=da_raw[h][:].rearrange("p j (m t) -> p t m j", t=PACK),
+            )
+
+        def quantize_da(h):
+            da_codes[h] = held("da_codes%d" % h, [P, KPASS], U32)
+            da_scales[h] = held("da_scales%d" % h, [P, KPASS], U8)
+            nc.vector.quantize_mx(out=da_codes[h][:].bitcast(FP8X4), scales=da_scales[h][:], in_=da_grouped[h][:])
+
+        def cast_fade():
+            nc.scalar.copy(out=fade32[:], in_=vec["fade"][:, 0, :])
+
         def warm_up(count):
             idle = bank()
             for i in range(count):
                 nc.tensor.matmul(idle[:], lhsT=zeros[:, :P], rhs=zeros[:], start=True, stop=True)
 
-        z_banks, z_grouped, z_codes, z_scales, z_pre, prev_pre = {}, {}, {}, {}, {}, {}
+        z_ordered, prev_ordered = {}, {}
 
         def order_words(raw, copy):
-            ordered = ring("z_pre", 4, [P, 2, TT * P], F32)
+            ordered = ring("staged", 4, [P, 2, PACK * P], F32)
             copy(
-                out=ordered[:].rearrange("p u (m i) -> p m u i", i=2),
-                in_=raw[:].bitcast(F32).rearrange("p a (m i u) -> p (a m) u i", i=2, u=2),
+                out=ordered[:].rearrange("r u (m i) -> r m u i", i=2),
+                in_=raw[:].bitcast(F32).rearrange("r a (m i u) -> r (a m) u i", i=2, u=2),
             )
             return ordered
 
-        def order_z(c, g, copy):
-            z_pre[c, g] = order_words(z_raw[c, g], copy)
+        def order_z(c, key):
+            z_ordered[c, key] = order_words(z_raw[c, key], on_vector)
 
-        def z_words(c, g, a, u):
-            if (c, g) in z_pre:
-                return z_pre[c, g][:, u, P * a : P * (a + 1)]
-            return z_raw[c, g][:].bitcast(F32)[:, a, u::2]
+        def order_prev(c):
+            prev_ordered[c] = order_words(prev_raw[c], on_scalar)
 
-        def turn_z_half(c, g, half):
+        def words(raw, ordered, piece, u):
+            if ordered is not None:
+                return ordered[:, u, P * piece : P * (piece + 1)]
+            flat = raw[:].bitcast(F32).rearrange("r a w -> r (a w)")
+            return flat[:, 2 * P * piece + u : 2 * P * (piece + 1) : 2]
+
+        z_banks, z_grouped, z_codes, z_scales = {}, {}, {}, {}
+
+        def turn_z(c, g, half):
             z_banks[c, g, half] = bank()
-            for a in range(2):
+            key = (c, ZA) if g == ZA else (c, half)
+            for j in range(2):
+                piece = 2 * half + j if g == ZA else 2 * j + g
                 for u in range(2):
-                    col = 2 * P * u + P * a
-                    nc.tensor.transpose(z_banks[c, g, half][:, col : col + P], z_words(c, g, 2 * half + a, u), ident[:])
+                    col = 2 * P * u + P * j
+                    nc.tensor.transpose(
+                        z_banks[c, g, half][:, col : col + P], words(z_raw[key], z_ordered.get(key), piece, u), ident[:]
+                    )
 
-        def turn_z(c, g):
-            for half in range(2):
-                turn_z_half(c, g, half)
-
-        def copy_z(c, g, half):
-            if half == 0:
-                z_grouped[c, g] = ring("bf_stage", 4, [P, PACK * CH], BF16)
-            dst = z_grouped[c, g][:].bitcast(F32)[:, CH * half : CH * (half + 1)]
-            nc.scalar.copy(
-                out=dst.rearrange("p (n u) -> p n u", u=2),
-                in_=z_banks[c, g, half][:].rearrange("p (u n) -> p n u", u=2),
+        def copy_z(c, g, half, copy):
+            if c not in z_grouped:
+                z_grouped[c] = ring("z_grouped", 2, [P, 3 * PACK * CH], BF16)
+            start = 2 * CH * g + CH * half
+            copy(
+                out=z_grouped[c][:].bitcast(F32)[:, start : start + CH].rearrange("p (r j u) -> p r j u", j=2, u=2),
+                in_=z_banks[c, g, half][:].rearrange("p (u j r) -> p r j u", j=2, u=2),
             )
 
-        def quantize_z(c, g, lo=0, hi=CH):
-            if lo == 0:
-                z_codes[c, g] = ring("z_codes", 6, [P, CH], U32)
-                z_scales[c, g] = ring("z_scales", 6, [P, CH], U8)
+        def quantize_z(c, first, end):
+            if c not in z_codes:
+                z_codes[c] = ring("z_codes", 2, [P, 3 * CH], U32)
+                z_scales[c] = ring("z_scales", 2, [P, 3 * CH], U8)
+            cols = slice(CH * first, CH * end)
             nc.vector.quantize_mx(
-                out=z_codes[c, g][:, lo:hi].bitcast(FP8X4), scales=z_scales[c, g][:, lo:hi],
-                in_=z_grouped[c, g][:, PACK * lo : PACK * hi],
+                out=z_codes[c][:, cols].bitcast(FP8X4), scales=z_scales[c][:, cols],
+                in_=z_grouped[c][:, PACK * CH * first : PACK * CH * end],
             )
 
-        s_banks, th, h_grouped, h_codes, h_scales = {}, {}, {}, {}, {}
+        s_banks, squashed, h_grouped, h_codes, h_scales = {}, {}, {}, {}, {}
+
+        def first_stage_pass(out, c, h, t, g, lo, hi):
+            cols = slice(P * t, P * (t + 1))
+            if g == ZA:
+                lhsT, lhsT_scale = da_codes[h][:, cols].bitcast(FP8X4), da_scales[h][:, cols]
+            else:
+                lhsT, lhsT_scale = dp_codes[h][:, g, 2 * P * t : 2 * P * (t + 1)].bitcast(FP4X4), scales[h][:, g, cols]
+            moving = slice(CH * g + lo, CH * g + hi)
+            nc.tensor.matmul_mx(
+                out=out, lhsT=lhsT, lhsT_scale=lhsT_scale,
+                rhs=z_codes[c][:, moving].bitcast(FP8X4), rhs_scale=z_scales[c][:, moving],
+                start=(g == 0), stop=(g == ZA),
+            )
 
         def correlate_pass(c, h, t, g):
             if g == 0:
                 s_banks[c, h, t] = bank()
-            cols = slice(P * t, P * (t + 1))
-            if g < 2:
-                lhsT = dp_codes[h][:, g, 2 * P * t : 2 * P * (t + 1)].bitcast(FP4X4)
-                lhsT_scale = dp_scales[h][:, g, cols]
-            else:
-                lhsT = da_codes[h][:, cols].bitcast(FP8X4)
-                lhsT_scale = da_scales[h][:, cols]
-            nc.tensor.matmul_mx(
-                out=s_banks[c, h, t][:], lhsT=lhsT, lhsT_scale=lhsT_scale,
-                rhs=z_codes[c, g][:].bitcast(FP8X4), rhs_scale=z_scales[c, g][:],
-                start=(g == 0), stop=(g == 2),
-            )
+            first_stage_pass(s_banks[c, h, t][:], c, h, t, g, 0, CH)
 
-        def correlate_group(c, h, t):
-            for g in range(3):
+        def correlate(c, h, t):
+            for g in range(ZA + 1):
                 correlate_pass(c, h, t, g)
-
-        def correlate(c, h):
-            for t in range(PACK):
-                for g in range(3):
-                    correlate_pass(c, h, t, g)
 
         def squash(c, h, t):
             if t == 0:
-                th[c, h] = ring("th", 2, [P, PACK, CH], F32)
-            nc.scalar.activation(out=th[c, h][:, t, :], in_=s_banks[c, h, t][:], func=ACT.Tanh)
+                squashed[c, h] = ring("squashed", 2, [P, PACK, CH], F32)
+            nc.scalar.activation(out=squashed[c, h][:, t, :], in_=s_banks[c, h, t][:], func=ACT.Tanh)
 
         def weigh(c, h):
             h_grouped[c, h] = ring("h_grouped", 2, [P, PACK * CH], BF16)
             nc.vector.tensor_tensor(
                 out=h_grouped[c, h][:].rearrange("p (n i t) -> p n t i", i=2, t=PACK),
-                in0=th[c, h][:].rearrange("p t (n i) -> p n t i", i=2),
-                in1=cw[:, h, :].unsqueeze(1).unsqueeze(3).to_broadcast([P, CH // 2, PACK, 2]),
+                in0=squashed[c, h][:].rearrange("p t (n i) -> p n t i", i=2),
+                in1=vec["cell_weight"][:, h, :].unsqueeze(1).unsqueeze(3).to_broadcast([P, HALF, PACK, 2]),
                 op=ALU.mult,
             )
 
-        def quantize_h(c, h):
-            h_codes[c, h] = ring("h_codes", 4, [P, CH], U32)
-            h_scales[c, h] = ring("h_scales", 4, [P, CH], U8)
-            nc.vector.quantize_mx(out=h_codes[c, h][:].bitcast(FP8X4), scales=h_scales[c, h][:], in_=h_grouped[c, h][:])
+        def quantize_h(c, h, lo, hi):
+            if lo == 0:
+                h_codes[c, h] = ring("h_codes", 4, [P, CH], U32)
+                h_scales[c, h] = ring("h_scales", 4, [P, CH], U8)
+            nc.vector.quantize_mx(
+                out=h_codes[c, h][:, lo:hi].bitcast(FP8X4), scales=h_scales[c, h][:, lo:hi],
+                in_=h_grouped[c, h][:, PACK * lo : PACK * hi],
+            )
+
+        tile_banks = {}
+
+        def correlate_tile(a):
+            tile_banks[a] = bank()
+            for t in range(PACK):
+                for g in range(ZA + 1):
+                    first_stage_pass(tile_banks[a][:, P * t : P * (t + 1)], LAST, 1, t, g, P * a, P * (a + 1))
+
+        def squash_tile(a):
+            if a == 0:
+                squashed[LAST, 1] = ring("squashed", 2, [P, CH, PACK], F32)
+            nc.scalar.activation(
+                out=squashed[LAST, 1][:, P * a : P * (a + 1), :],
+                in_=tile_banks[a][:].rearrange("p (t n) -> p n t", t=PACK), func=ACT.Tanh,
+            )
+
+        def weigh_tiles(lo, hi):
+            if lo == 0:
+                h_grouped[LAST, 1] = ring("h_grouped", 2, [P, PACK * CH], BF16)
+            nc.vector.tensor_tensor(
+                out=h_grouped[LAST, 1][:, PACK * lo : PACK * hi].rearrange("p (n t) -> p n t", t=PACK),
+                in0=squashed[LAST, 1][:, lo:hi, :],
+                in1=vec["cell_weight"][:, 1, :].unsqueeze(1).to_broadcast([P, hi - lo, PACK]),
+                op=ALU.mult,
+            )
 
         prev_banks, faded, f_banks, y_zones = {}, {}, {}, {}
 
-        def order_prev(c, copy):
-            prev_pre[c] = order_words(prev_raw[c], copy)
-
-        def turn_prev_half(c, u):
+        def turn_prev(c, u):
             prev_banks[c, u] = bank()
-            for a in range(TT):
-                words = prev_pre[c][:, u, P * a : P * (a + 1)] if c in prev_pre else prev_raw[c][:].bitcast(F32)[:, a, u::2]
-                nc.tensor.transpose(prev_banks[c, u][:, P * a : P * (a + 1)], words, ident[:])
-
-        def turn_prev(c):
-            for u in range(2):
-                turn_prev_half(c, u)
+            for piece in range(PACK):
+                nc.tensor.transpose(
+                    prev_banks[c, u][:, P * piece : P * (piece + 1)], words(prev_raw[c], prev_ordered[c], piece, u), ident[:]
+                )
 
         def fade_prev(c, t):
             if t == 0:
                 faded[c] = ring("faded", 2, [P, PACK, CH], F32)
-            pair = prev_banks[c, t // 2][:].bitcast(BF16).rearrange("p (n e) -> p e n", e=2)
+            pairs = prev_banks[c, t // 2][:].bitcast(BF16).rearrange("p (a j r e) -> p e a r j", a=2, j=2, e=2)
             nc.scalar.activation(
-                out=faded[c][:, t, :], in_=pair[:, t % 2, :], func=ACT.Identity,
-                scale=fade32[:, t : t + 1], bias=vec["bias"][:, 0, t : t + 1],
+                out=faded[c][:, t, :].rearrange("p (a r j) -> p a r j", a=2, j=2), in_=pairs[:, t % 2],
+                func=ACT.Identity, scale=fade32[:, t : t + 1], bias=vec["bias"][:, 0, t : t + 1],
             )
 
-        def fuse_pass(c, t, h):
-            if h == 0:
-                f_banks[c, t] = bank()
-            cols = slice(P * t, P * (t + 1))
-            nc.tensor.matmul_mx(
-                out=f_banks[c, t][:], lhsT=w_codes[:, h, cols].bitcast(FP8X4), lhsT_scale=w_scales[:, h, cols],
-                rhs=h_codes[c, h][:].bitcast(FP8X4), rhs_scale=h_scales[c, h][:],
-                start=(h == 0), stop=(h == 1),
-            )
+        def in_bank(lo, hi, b):
+            width = hi - lo
+            return [(CH // width * b + i, slice(width * i, width * (i + 1))) for i in range(CH // width)]
 
-        def fuse_group(c, t):
-            for h in range(2):
-                fuse_pass(c, t, h)
-
-        def fuse(c):
-            for t in range(PACK):
-                for h in range(2):
-                    fuse_pass(c, t, h)
-
-        def join(c, t):
-            if t == 0:
-                y_zones[c] = ring("y_zones", 2, [P, PACK, CH], F32)
-            nc.vector.scalar_tensor_tensor(
-                out=y_zones[c][:, t, :], in0=f_banks[c, t][:], scalar=vec["gain"][:, 0, t : t + 1],
-                in1=faded[c][:, t, :], op0=ALU.mult, op1=ALU.add,
-            )
-
-        y_banks, y_rows, y_grouped = {}, {}, {}
-        y_codes = held("y_codes", [P, T], U32)
-        y_scales = held("y_scales", [P, T], U8)
-
-        def turn_y_tile(c, a):
-            y_banks[c, a] = bank()
-            for t in range(PACK):
-                nc.tensor.transpose(
-                    y_banks[c, a][:, P * t : P * (t + 1)], y_zones[c][:, t, P * a : P * (a + 1)], ident[:]
-                )
-
-        def turn_y(c):
-            for a in range(TT):
-                turn_y_tile(c, a)
-
-        def copy_y(c, a, engine):
-            y_rows[c, a] = ring("y_rows", 6, [P, N], F32)
-            dst = y_rows[c, a][:].rearrange("q (p t) -> q p t", t=PACK)
-            src = y_banks[c, a][:].rearrange("q (t p) -> q p t", t=PACK)
-            if engine == "vector":
-                nc.vector.tensor_copy(out=dst, in_=src)
-            else:
-                nc.scalar.copy(out=dst, in_=src)
-            row = CH * c + P * a
-            nc.sync.dma_start(out=out_0[row : row + P, :], in_=y_rows[c, a][:])
-
-        def group_y(c, copy):
-            y_grouped[c] = ring("bf_stage", 4, [P, PACK * CH], BF16)
-            copy(
-                out=y_grouped[c][:].rearrange("p (n i t) -> p n t i", i=2, t=PACK),
-                in_=y_zones[c][:].rearrange("p t (n i) -> p n t i", i=2),
-            )
-
-        def quantize_y(c):
-            cols = slice(CH * c, CH * (c + 1))
-            nc.vector.quantize_mx(out=y_codes[:, cols].bitcast(FP8X4), scales=y_scales[:, cols], in_=y_grouped[c][:])
-            nc.sync.dma_start(
-                out=out_1[0, :, cols, :].rearrange("p m t -> p (m t)").bitcast(I32), in_=y_codes[:, cols].bitcast(I32)
-            )
-
-        def store_y_scales(cols):
-            for q in range(4):
-                nc.sync.dma_start(
-                    out=out_2[0, 4 * q : 4 * q + 4, cols].bitcast(I32), in_=y_scales[32 * q : 32 * q + 4, cols].bitcast(I32)
-                )
-
-        tile_banks, tile_th, tile_grouped, tile_f, tile_y = {}, {}, {}, {}, {}
-
-        def correlate_tile(c, h, a):
-            tile_banks[a] = bank()
-            toks = slice(P * a, P * (a + 1))
-            for t in range(PACK):
-                cols = slice(P * t, P * (t + 1))
-                for g in range(3):
-                    if g < 2:
-                        lhsT = dp_codes[h][:, g, 2 * P * t : 2 * P * (t + 1)].bitcast(FP4X4)
-                        lhsT_scale = dp_scales[h][:, g, cols]
-                    else:
-                        lhsT = da_codes[h][:, cols].bitcast(FP8X4)
-                        lhsT_scale = da_scales[h][:, cols]
-                    nc.tensor.matmul_mx(
-                        out=tile_banks[a][:, cols], lhsT=lhsT, lhsT_scale=lhsT_scale,
-                        rhs=z_codes[c, g][:, toks].bitcast(FP8X4), rhs_scale=z_scales[c, g][:, toks],
-                        start=(g == 0), stop=(g == 2),
-                    )
-
-        def squash_tile(a):
-            tile_th[a] = ring("tile_th", 2, [P, P * PACK], F32)
-            nc.scalar.activation(
-                out=tile_th[a][:].rearrange("p (n t) -> p n t", t=PACK),
-                in_=tile_banks[a][:].rearrange("p (t n) -> p n t", t=PACK), func=ACT.Tanh,
-            )
-
-        def weigh_tile(h, a):
-            tile_grouped[a] = ring("tile_grouped", 2, [P, P * PACK], BF16)
-            nc.vector.tensor_tensor(
-                out=tile_grouped[a][:].rearrange("p (n t) -> p n t", t=PACK),
-                in0=tile_th[a][:].rearrange("p (n t) -> p n t", t=PACK),
-                in1=cw[:, h, :].unsqueeze(1).to_broadcast([P, P, PACK]),
-                op=ALU.mult,
-            )
-
-        def quantize_h_tile(c, h, a):
-            if a == 0:
-                h_codes[c, h] = ring("h_codes", 4, [P, CH], U32)
-                h_scales[c, h] = ring("h_scales", 4, [P, CH], U8)
-            toks = slice(P * a, P * (a + 1))
-            nc.vector.quantize_mx(
-                out=h_codes[c, h][:, toks].bitcast(FP8X4), scales=h_scales[c, h][:, toks], in_=tile_grouped[a][:]
-            )
-
-        def fuse_tile(c, a):
-            tile_f[a] = bank()
-            toks = slice(P * a, P * (a + 1))
-            for t in range(PACK):
+        def fuse(c, lo, hi, b):
+            f_banks[c, lo, b] = bank()
+            for t, place in in_bank(lo, hi, b):
                 cols = slice(P * t, P * (t + 1))
                 for h in range(2):
                     nc.tensor.matmul_mx(
-                        out=tile_f[a][:, cols], lhsT=w_codes[:, h, cols].bitcast(FP8X4), lhsT_scale=w_scales[:, h, cols],
-                        rhs=h_codes[c, h][:, toks].bitcast(FP8X4), rhs_scale=h_scales[c, h][:, toks],
+                        out=f_banks[c, lo, b][:, place],
+                        lhsT=w_codes[:, h, cols].bitcast(FP8X4), lhsT_scale=scales[1][W_ROW:P, h, cols],
+                        rhs=h_codes[c, h][:, lo:hi].bitcast(FP8X4), rhs_scale=h_scales[c, h][:, lo:hi],
                         start=(h == 0), stop=(h == 1),
                     )
 
-        def join_tile(c, a):
-            if a == 0:
+        def join(c, lo, hi, b):
+            if c not in y_zones:
                 y_zones[c] = ring("y_zones", 2, [P, PACK, CH], F32)
-            toks = slice(P * a, P * (a + 1))
-            for t in range(PACK):
+            for t, place in in_bank(lo, hi, b):
                 nc.vector.scalar_tensor_tensor(
-                    out=y_zones[c][:, t, toks], in0=tile_f[a][:, P * t : P * (t + 1)], scalar=vec["gain"][:, 0, t : t + 1],
-                    in1=faded[c][:, t, toks], op0=ALU.mult, op1=ALU.add,
+                    out=y_zones[c][:, t, lo:hi], in0=f_banks[c, lo, b][:, place],
+                    scalar=vec["gain"][:, 0, t : t + 1], in1=faded[c][:, t, lo:hi], op0=ALU.mult, op1=ALU.add,
                 )
 
-        def group_y_tile(c, a, copy):
-            tile_y[a] = ring("tile_y", 2, [P, P * PACK], BF16)
+        y_banks, y_grouped = {}, {}
+        y_codes = held("y_codes", [P, T], U32)
+        y_scales = held("y_scales", [P, T], U8)
+
+        def turn_y(c, a):
+            y_banks[c, a] = bank()
+            for t in range(PACK):
+                nc.tensor.transpose(y_banks[c, a][:, P * t : P * (t + 1)], y_zones[c][:, t, P * a : P * (a + 1)], ident[:])
+
+        def copy_y(c, a):
+            rows = ring("y_rows", 5, [P, N], F32)
+            nc.scalar.copy(
+                out=rows[:].rearrange("n (p t) -> n p t", t=PACK),
+                in_=y_banks[c, a][:].rearrange("n (t p) -> n p t", t=PACK),
+            )
+            row = CH * c + P * a
+            nc.sync.dma_start(out=out_0[row : row + P, :], in_=rows[:])
+
+        def group_y(c, lo, hi, copy):
+            if lo == 0:
+                y_grouped[c] = ring("y_grouped", 2, [P, PACK * CH], BF16)
             copy(
-                out=tile_y[a][:].rearrange("p (n i t) -> p n t i", i=2, t=PACK),
-                in_=y_zones[c][:, :, P * a : P * (a + 1)].rearrange("p t (n i) -> p n t i", i=2),
+                out=y_grouped[c][:, PACK * lo : PACK * hi].rearrange("p (n i t) -> p n t i", i=2, t=PACK),
+                in_=y_zones[c][:, :, lo:hi].rearrange("p t (n i) -> p n t i", i=2),
             )
 
-        def quantize_y_tile(c, a):
-            cols = slice(CH * c + P * a, CH * c + P * (a + 1))
-            nc.vector.quantize_mx(out=y_codes[:, cols].bitcast(FP8X4), scales=y_scales[:, cols], in_=tile_y[a][:])
+        def quantize_y(c, lo, hi):
+            cols = slice(CH * c + lo, CH * c + hi)
+            nc.vector.quantize_mx(
+                out=y_codes[:, cols].bitcast(FP8X4), scales=y_scales[:, cols], in_=y_grouped[c][:, PACK * lo : PACK * hi]
+            )
 
-        def store_y_codes(cols):
+        def store_y_codes(c, lo, hi):
+            cols = slice(CH * c + lo, CH * c + hi)
             nc.sync.dma_start(
                 out=out_1[0, :, cols, :].rearrange("p m t -> p (m t)").bitcast(I32), in_=y_codes[:, cols].bitcast(I32)
             )
 
+        def store_y_scales(lo, hi):
+            for q in range(4):
+                nc.sync.dma_start(
+                    out=out_2[0, 4 * q : 4 * q + 4, lo:hi].bitcast(I32),
+                    in_=y_scales[32 * q : 32 * q + 4, lo:hi].bitcast(I32),
+                )
+
+
+        warm_up(WARM_FIRST)
         order_scales(0)
-        warm_up(7)
-        turn_z_half(0, 0, 0)
-        turn_z_half(0, 0, 1)
-        warm_up(2)
+        turn_z(0, 1, 0)
         order_dp(0)
-        turn_z_half(0, 1, 0)
-        order_scales(1)
-        copy_z(0, 0, 0)
-        copy_z(0, 0, 1)
-        turn_z_half(0, 1, 1)
-        copy_z(0, 1, 0)
-        quantize_z(0, 0)
-        turn_z_half(0, 2, 0)
-        copy_z(0, 1, 1)
-        turn_z_half(0, 2, 1)
-        copy_z(0, 2, 0)
-        quantize_z(0, 1)
+        turn_z(0, 0, 0)
+        warm_up(WARM_BETWEEN)
+        copy_z(0, 1, 0, on_vector)
+        turn_z(0, 0, 1)
+        copy_z(0, 0, 0, on_scalar)
+        turn_z(0, 1, 1)
+        copy_z(0, 0, 1, on_vector)
+        copy_z(0, 1, 1, on_scalar)
+        quantize_z(0, 0, 1)
+        turn_z(0, 2, 0)
+        turn_z(0, 2, 1)
+        quantize_z(0, 1, 2)
+        group_da_on_vector(0)
         correlate_pass(0, 0, 0, 0)
-        group_da(0, nc.vector.tensor_copy)
-        copy_z(0, 2, 1)
-        quantize_z(0, 2)
+        copy_z(0, 2, 0, on_scalar)
         correlate_pass(0, 0, 1, 0)
-        quantize_da(0)
         correlate_pass(0, 0, 0, 1)
-        group_da(1, nc.scalar.copy)
         correlate_pass(0, 0, 1, 1)
-        order_dp(1)
-        order_z(1, 1, nc.vector.tensor_copy)
+        copy_z(0, 2, 1, on_scalar)
+        quantize_z(0, 2, 3)
         correlate_pass(0, 0, 2, 0)
+        quantize_da(0)
         correlate_pass(0, 0, 3, 0)
         correlate_pass(0, 0, 2, 1)
-        correlate_pass(0, 0, 3, 1)
         correlate_pass(0, 0, 0, 2)
+        correlate_pass(0, 0, 3, 1)
+        group_da_on_scalar(1)
         correlate_pass(0, 0, 1, 2)
-        squash(0, 0, 0)
-        quantize_da(1)
         correlate_pass(0, 0, 2, 2)
         correlate_pass(0, 0, 3, 2)
-        turn_z_half(1, 0, 0)
-        order_z(1, 2, nc.vector.tensor_copy)
-        turn_z_half(1, 0, 1)
+        order_dp(1)
+        turn_z(1, 0, 0)
+        squash(0, 0, 0)
         squash(0, 0, 1)
-        correlate_group(0, 1, 0)
         squash(0, 0, 2)
+        turn_z(1, 1, 0)
+        quantize_da(1)
         squash(0, 0, 3)
-        correlate_group(0, 1, 1)
-        turn_z_half(1, 2, 0)
-        turn_z_half(1, 1, 0)
-        weigh(0, 0)
-        copy_z(1, 0, 0)
-        copy_z(1, 0, 1)
+        order_scales(1)
+        order_prev(0)
+        correlate(0, 1, 0)
+        turn_z(1, 1, 1)
+        turn_z(1, 0, 1)
         squash(0, 1, 0)
-        squash(0, 1, 1)
-        turn_z_half(1, 1, 1)
-        copy_z(1, 2, 0)
+        copy_z(1, 0, 0, on_vector)
+        turn_prev(0, 0)
+        correlate(0, 1, 1)
         cast_fade()
-        copy_z(1, 1, 0)
-        copy_z(1, 1, 1)
-        correlate_group(0, 1, 2)
-        order_w_scales()
-        quantize_h(0, 0)
-        quantize_z(1, 0)
-        turn_z_half(1, 2, 1)
-        turn_prev_half(0, 0)
-        copy_z(1, 2, 1)
-        quantize_z(1, 1)
+        copy_z(1, 1, 0, on_scalar)
+        weigh(0, 0)
         fade_prev(0, 0)
-        squash(0, 1, 2)
-        quantize_z(1, 2)
-        turn_prev_half(0, 1)
-        correlate_group(0, 1, 3)
-        squash(0, 1, 3)
-        fade_prev(0, 1)
+        copy_z(1, 0, 1, on_scalar)
+        turn_z(1, 2, 0)
+        copy_z(1, 1, 1, on_vector)
         order_w()
+        turn_z(1, 2, 1)
+        quantize_z(1, 1, 2)
+        fade_prev(0, 1)
+        copy_z(1, 2, 0, on_vector)
+        copy_z(1, 2, 1, on_scalar)
+        turn_prev(0, 1)
+        correlate(0, 1, 2)
+        quantize_z(1, 0, 1)
+        squash(0, 1, 1)
+        correlate(0, 1, 3)
+        quantize_z(1, 2, 3)
+        quantize_h(0, 0, 0, CH)
+        squash(0, 1, 2)
         fade_prev(0, 2)
+        squash(0, 1, 3)
         fade_prev(0, 3)
-        for c in (1, 2):
-            order_z(c + 1, 0, nc.vector.tensor_copy)
+
+        for c in range(1, LAST):
+            correlate(c, 0, 0)
+            order_prev(c)
+            correlate(c, 0, 1)
+            correlate(c, 0, 2)
             if c >= 2:
-                copy_y(c - 2, 0, 'scalar')
+                copy_y(c - 2, 0)
+            order_z(c + 1, 1)
+            order_z(c + 1, 0)
             if c >= 2:
-                copy_y(c - 2, 1, 'scalar')
-            correlate_group(c, 0, 0)
-            correlate_group(c, 0, 1)
-            if c >= 2:
-                copy_y(c - 2, 2, 'scalar')
-            correlate_group(c, 0, 2)
-            correlate_group(c, 0, 3)
-            turn_z_half(c + 1, 0, 0)
-            weigh(c - 1, 1)
+                copy_y(c - 2, 1)
+                copy_y(c - 2, 2)
             squash(c, 0, 0)
-            turn_z_half(c + 1, 0, 1)
+            turn_z(c + 1, 1, 0)
+            turn_z(c + 1, 0, 0)
+            turn_z(c + 1, 1, 1)
+            correlate(c, 0, 3)
+            if c >= 2:
+                copy_y(c - 2, 3)
             squash(c, 0, 1)
-            order_z(c + 1, 1, nc.vector.tensor_copy)
-            turn_z_half(c + 1, 1, 0)
-            quantize_h(c - 1, 1)
-            if c >= 2:
-                copy_y(c - 2, 3, 'scalar')
-            order_z(c + 1, 2, nc.vector.tensor_copy)
             squash(c, 0, 2)
-            turn_z_half(c + 1, 1, 1)
-            fuse_group(c - 1, 0)
+            weigh(c - 1, 1)
             squash(c, 0, 3)
-            copy_z(c + 1, 0, 0)
-            fuse_group(c - 1, 1)
-            copy_z(c + 1, 0, 1)
-            fuse_group(c - 1, 2)
-            fuse_group(c - 1, 3)
-            copy_z(c + 1, 1, 0)
-            order_prev(c, nc.scalar.copy)
-            turn_z_half(c + 1, 2, 0)
-            weigh(c, 0)
-            join(c - 1, 0)
-            turn_z_half(c + 1, 2, 1)
-            join(c - 1, 1)
-            copy_z(c + 1, 1, 1)
-            turn_prev_half(c, 0)
-            join(c - 1, 2)
-            copy_z(c + 1, 2, 0)
-            turn_prev_half(c, 1)
-            correlate_group(c, 1, 0)
-            correlate_group(c, 1, 1)
-            copy_z(c + 1, 2, 1)
-            quantize_z(c + 1, 0)
-            join(c - 1, 3)
-            quantize_z(c + 1, 1)
-            correlate_group(c, 1, 2)
-            correlate_group(c, 1, 3)
+            copy_z(c + 1, 1, 0, on_scalar)
+            order_z(c + 1, 2)
+            copy_z(c + 1, 0, 0, on_scalar)
+            turn_prev(c, 0)
+            copy_z(c + 1, 1, 1, on_vector)
+            quantize_h(c - 1, 1, 0, CH)
+            turn_z(c + 1, 2, 0)
             fade_prev(c, 0)
-            squash(c, 1, 0)
-            if c >= 2:
-                quantize_y(c - 2)
-            quantize_z(c + 1, 2)
+            turn_z(c + 1, 0, 1)
             fade_prev(c, 1)
-            group_y(c - 1, nc.vector.tensor_copy)
-            turn_y_tile(c - 1, 0)
-            turn_y_tile(c - 1, 1)
+            copy_z(c + 1, 2, 0, on_scalar)
+            correlate(c, 1, 0)
+            fuse(c - 1, 0, CH, 0)
+            weigh(c, 0)
+            fuse(c - 1, 0, CH, 1)
+            turn_prev(c, 1)
+            turn_z(c + 1, 2, 1)
+            join(c - 1, 0, CH, 0)
+            join(c - 1, 0, CH, 1)
+            copy_z(c + 1, 0, 1, on_scalar)
+            squash(c, 1, 0)
+            fuse(c - 1, 0, CH, 2)
+            copy_z(c + 1, 2, 1, on_scalar)
+            fuse(c - 1, 0, CH, 3)
+            quantize_h(c, 0, 0, CH)
+            quantize_z(c + 1, 0, 2)
             fade_prev(c, 2)
+            correlate(c, 1, 1)
+            join(c - 1, 0, CH, 2)
+            correlate(c, 1, 2)
+            correlate(c, 1, 3)
             fade_prev(c, 3)
+            join(c - 1, 0, CH, 3)
             squash(c, 1, 1)
-            turn_y_tile(c - 1, 2)
-            turn_y_tile(c - 1, 3)
+            quantize_z(c + 1, 2, 3)
+            if c >= 2:
+                quantize_y(c - 2, 0, CH)
+                store_y_codes(c - 2, 0, CH)
+            turn_y(c - 1, 0)
+            turn_y(c - 1, 1)
             squash(c, 1, 2)
             squash(c, 1, 3)
-            quantize_h(c, 0)
-        copy_y(1, 0, 'scalar')
-        correlate_group(3, 0, 0)
-        copy_y(1, 1, 'scalar')
-        order_prev(3, nc.vector.tensor_copy)
-        correlate_group(3, 0, 1)
-        copy_y(1, 2, 'scalar')
-        correlate_group(3, 0, 2)
-        weigh(2, 1)
-        copy_y(1, 3, 'scalar')
-        turn_prev_half(3, 0)
-        squash(3, 0, 0)
-        squash(3, 0, 1)
-        fade_prev(3, 0)
-        squash(3, 0, 2)
-        turn_prev_half(3, 1)
-        quantize_h(2, 1)
-        correlate_group(3, 0, 3)
-        fuse_group(2, 0)
-        fuse_group(2, 1)
-        fuse_group(2, 2)
-        quantize_y(1)
-        join(2, 0)
-        fuse_group(2, 3)
-        join(2, 1)
-        fade_prev(3, 1)
-        correlate_tile(3, 1, 0)
-        join(2, 2)
-        fade_prev(3, 2)
-        join(2, 3)
-        correlate_tile(3, 1, 1)
-        fade_prev(3, 3)
-        turn_y_tile(2, 0)
-        squash(3, 0, 3)
+            turn_y(c - 1, 2)
+            turn_y(c - 1, 3)
+            group_y(c - 1, 0, CH, on_vector)
+
+        copy_y(LAST - 2, 0)
+        order_prev(LAST)
+        correlate(LAST, 0, 0)
+        squash(LAST, 0, 0)
+        correlate(LAST, 0, 1)
+        copy_y(LAST - 2, 1)
+        weigh(LAST - 1, 1)
+        copy_y(LAST - 2, 2)
+        correlate(LAST, 0, 2)
+        quantize_h(LAST - 1, 1, 0, CH)
+        correlate(LAST, 0, 3)
+        turn_prev(LAST, 0)
+        copy_y(LAST - 2, 3)
+        turn_prev(LAST, 1)
+        squash(LAST, 0, 1)
+        quantize_y(LAST - 2, 0, CH)
+        store_y_codes(LAST - 2, 0, CH)
+        fuse(LAST - 1, 0, CH, 0)
+        squash(LAST, 0, 2)
+        fuse(LAST - 1, 0, CH, 1)
+        join(LAST - 1, 0, CH, 0)
+        fuse(LAST - 1, 0, CH, 2)
+        join(LAST - 1, 0, CH, 1)
+        squash(LAST, 0, 3)
+        correlate_tile(0)
+        join(LAST - 1, 0, CH, 2)
+        fuse(LAST - 1, 0, CH, 3)
+        fade_prev(LAST, 0)
+        fade_prev(LAST, 1)
+        fade_prev(LAST, 2)
+        weigh(LAST, 0)
+        join(LAST - 1, 0, CH, 3)
+        fade_prev(LAST, 3)
+        correlate_tile(1)
         squash_tile(0)
-        weigh(3, 0)
-        turn_y_tile(2, 1)
+        quantize_h(LAST, 0, 0, CH)
         squash_tile(1)
-        turn_y_tile(2, 2)
-        weigh_tile(1, 0)
-        copy_y(2, 0, 'scalar')
-        copy_y(2, 1, 'scalar')
-        quantize_h(3, 0)
-        turn_y_tile(2, 3)
-        copy_y(2, 2, 'scalar')
-        correlate_tile(3, 1, 2)
+        correlate_tile(2)
         squash_tile(2)
-        copy_y(2, 3, 'scalar')
-        weigh_tile(1, 1)
-        quantize_h_tile(3, 1, 0)
-        correlate_tile(3, 1, 3)
-        fuse_tile(3, 0)
-        quantize_h_tile(3, 1, 1)
-        weigh_tile(1, 2)
+        turn_y(LAST - 1, 0)
+        copy_y(LAST - 1, 0)
+        correlate_tile(3)
         squash_tile(3)
-        join_tile(3, 0)
-        quantize_h_tile(3, 1, 2)
-        fuse_tile(3, 1)
-        group_y(2, nc.scalar.copy)
-        join_tile(3, 1)
-        weigh_tile(1, 3)
-        turn_y_tile(3, 0)
-        fuse_tile(3, 2)
-        group_y_tile(3, 0, nc.vector.tensor_copy)
-        turn_y_tile(3, 1)
-        copy_y(3, 0, 'scalar')
-        copy_y(3, 1, 'scalar')
-        quantize_h_tile(3, 1, 3)
-        join_tile(3, 2)
-        quantize_y(2)
-        fuse_tile(3, 3)
-        join_tile(3, 3)
-        turn_y_tile(3, 2)
-        group_y_tile(3, 1, nc.vector.tensor_copy)
-        turn_y_tile(3, 3)
-        copy_y(3, 2, 'scalar')
-        quantize_y_tile(3, 0)
-        group_y_tile(3, 2, nc.vector.tensor_copy)
-        quantize_y_tile(3, 1)
-        group_y_tile(3, 3, nc.vector.tensor_copy)
-        quantize_y_tile(3, 2)
-        quantize_y_tile(3, 3)
-        copy_y(3, 3, 'scalar')
-        store_y_codes(slice(1536, 2048))
-        store_y_scales(slice(0, 2048))
+        weigh_tiles(0, HALF)
+        group_y(LAST - 1, 0, HALF, on_scalar)
+        turn_y(LAST - 1, 1)
+        turn_y(LAST - 1, 2)
+        group_y(LAST - 1, HALF, CH, on_vector)
+        turn_y(LAST - 1, 3)
+        copy_y(LAST - 1, 1)
+        quantize_h(LAST, 1, 0, HALF)
+        weigh_tiles(HALF, CH)
+        fuse(LAST, 0, HALF, 0)
+        quantize_y(LAST - 1, 0, CH)
+        quantize_h(LAST, 1, HALF, CH)
+        fuse(LAST, 0, HALF, 1)
+        fuse(LAST, HALF, CH, 0)
+        copy_y(LAST - 1, 2)
+        store_y_scales(0, LAST * CH)
+        store_y_codes(LAST - 1, 0, CH)
+        fuse(LAST, HALF, CH, 1)
+        join(LAST, 0, HALF, 0)
+        copy_y(LAST - 1, 3)
+        join(LAST, 0, HALF, 1)
+        join(LAST, HALF, CH, 0)
+        turn_y(LAST, 0)
+        join(LAST, HALF, CH, 1)
+        turn_y(LAST, 1)
+        copy_y(LAST, 0)
+        turn_y(LAST, 2)
+        copy_y(LAST, 1)
+        turn_y(LAST, 3)
+        group_y(LAST, 0, HALF, on_vector)
+        quantize_y(LAST, 0, HALF)
+        group_y(LAST, HALF, CH, on_vector)
+        quantize_y(LAST, HALF, CH)
+        copy_y(LAST, 2)
+        copy_y(LAST, 3)
+        store_y_codes(LAST, 0, HALF)
+        store_y_codes(LAST, HALF, CH)
+        store_y_scales(LAST * CH, T)

from contextlib import ExitStack

import concourse.mybir as mybir
from concourse.masks import make_identity

T, KA, KP, G, N = 2048, 512, 1024, 1024, 512
FLOPS = 2 * T * G * (KA + KP) + 2 * T * G * N

F32 = mybir.dt.float32
BF16 = mybir.dt.bfloat16
I32 = mybir.dt.int32
U32 = mybir.dt.uint32
U8 = mybir.dt.uint8
FP8X4 = mybir.dt.float8_e4m3fn_x4
FP4X4 = mybir.dt.float4_e2m1fn_x4
ACT = mybir.ActivationFunctionType
ALU = mybir.AluOpType

P = 128
PACK = 4
KPASS = P * PACK
CH = 512
HALF = CH // 2
LAST = T // CH - 1
BANKS = 8
ZA = 2
W_ROW = 4
WARM_FIRST, WARM_BETWEEN = 7, 2


def tile_multistatic_range_fusion_k6_kernel(
    tc, za, da, zp, passive_words, passive_scales, cell_weight, fuse_words, fuse_scales,
    zone_gain, fade, prev, bias, out_0, out_1, out_2,
):
    nc = tc.nc
    on_vector, on_scalar = nc.vector.tensor_copy, nc.scalar.copy
    with ExitStack() as ctx:
        sbuf = ctx.enter_context(tc.tile_pool(name="sbuf", bufs=1))
        psum = ctx.enter_context(tc.psum_pool(name="psum", bufs=1))
        ctx.enter_context(tc.manual_schedule())

        turns = {}

        def next_turn(name):
            turns[name] = turns.get(name, -1) + 1
            return turns[name]

        def held(name, shape, dtype):
            return sbuf.tile(shape, dtype, name=name, tag=name, align_bytes=64)

        def ring(name, depth, shape, dtype):
            return held("%s%d" % (name, next_turn(name) % depth), shape, dtype)

        def bank():
            return psum.tile([P, CH], F32, name="bank", tag="bank%d" % (next_turn("bank") % BANKS))

        scale_raw = held("scale_raw", [P, 2, G], U8)
        nc.vector.memset(scale_raw[:].rearrange("p g n -> p (g n)").bitcast(I32), 0)
        zeros = held("zeros", [P, CH], BF16)
        nc.gpsimd.memset(zeros[:], 0.0)
        ident = held("ident", [P, P], F32)
        make_identity(nc, ident[:])

        def load_scale_rows(queue, src, row, cols):
            for q in range(4):
                queue.dma_start(
                    out=scale_raw[32 * q + row : 32 * q + row + 4, :, cols].bitcast(I32),
                    in_=src[:, 4 * q : 4 * q + 4, :].rearrange("g r n -> r g n").bitcast(I32),
                )

        load_scale_rows(nc.scalar, passive_scales, 0, slice(0, G))
        table_warm = held("table_warm", [P, 8], F32)
        nc.scalar.activation(out=table_warm[:], in_=zeros[:, :8], func=ACT.Tanh)

        dp_raw, da_raw, z_raw, prev_raw, vec = {}, {}, {}, {}, {}

        def load_dp(h):
            dp_raw[h] = held("dp_raw%d" % h, [P, 2, 2 * KPASS], U8)
            src = passive_words[:, :, 2 * KPASS * h : 2 * KPASS * (h + 1)]
            nc.sync.dma_start(out=dp_raw[h][:].bitcast(I32), in_=src.rearrange("g p n -> p g n").bitcast(I32))

        def load_da(h):
            da_raw[h] = ring("staged", 4, [P, PACK, KPASS], BF16)
            src = da[:, KPASS * h : KPASS * (h + 1)]
            nc.sync.dma_start(out=da_raw[h][:], in_=src.rearrange("(p j) n -> p j n", j=PACK))

        def load_zp(c, half):
            row = CH * c + HALF * half
            z_raw[c, half] = held("z_raw%d_%d" % (c, half), [P, 2, KP], BF16)
            nc.sync.dma_start(out=z_raw[c, half][:], in_=zp[row : row + HALF, :].rearrange("(r j) k -> r j k", j=2))

        def chunk_rows(src, c):
            return src[CH * c : CH * (c + 1), :].rearrange("(a r j) k -> r a (j k)", a=2, j=2)

        def load_za(c, halves):
            if (c, ZA) not in z_raw:
                z_raw[c, ZA] = held("z_raw%d_%d" % (c, ZA), [P, 2, 2 * KA], BF16)
            nc.sync.dma_start(out=z_raw[c, ZA][:, halves, :], in_=chunk_rows(za, c)[:, halves, :])

        def load_prev(c):
            prev_raw[c] = held("prev_raw" if c == 0 else "z_raw0_%d" % (c - 1), [P, 2, 2 * N], BF16)
            nc.sync.dma_start(out=prev_raw[c][:], in_=chunk_rows(prev, c))

        def load_vector(name, src):
            groups = src.shape[0] // KPASS
            vec[name] = held(name, [P, groups, PACK], BF16)
            nc.sync.dma_start(out=vec[name][:], in_=src.rearrange("(h p t) -> p h t", h=groups, t=PACK))

        w_raw = held("w_raw", [P, 2, N], U32)

        load_zp(0, 0)
        load_dp(0)
        load_zp(0, 1)
        load_za(0, slice(0, 1))
        load_za(0, slice(1, 2))
        load_da(0)
        load_da(1)
        load_vector("bias", bias)
        load_vector("fade", fade)
        load_dp(1)
        load_zp(1, 0)
        load_scale_rows(nc.sync, fuse_scales, W_ROW, slice(KPASS, G))
        load_prev(0)
        load_vector("cell_weight", cell_weight)
        load_zp(1, 1)
        load_vector("gain", zone_gain)
        nc.sync.dma_start(out=w_raw[:].bitcast(I32), in_=fuse_words.rearrange("g p n t -> p g (n t)").bitcast(I32))
        load_za(1, slice(0, 2))
        for c in range(2, LAST + 1):
            load_zp(c, 0)
            load_zp(c, 1)
            load_za(c, slice(0, 2))
            load_prev(c - 1)
        load_prev(LAST)

        dp_codes, scales, da_grouped, da_codes, da_scales = {}, {}, {}, {}, {}
        w_codes = held("w_codes", [P, 2, N], U32)
        fade32 = held("fade32", [P, PACK], F32)

        def order_dp(h):
            dp_codes[h] = held("dp_codes%d" % h, [P, 2, 2 * KPASS], U8)
            for g in range(2):
                nc.vector.tensor_copy(
                    out=dp_codes[h][:, g, :].rearrange("p (t m b) -> p t m b", t=PACK, b=2),
                    in_=dp_raw[h][:, g, :].rearrange("p (m t b) -> p t m b", t=PACK, b=2),
                )

        def order_scales(h):
            scales[h] = held("scales%d" % h, [P, 2, KPASS], U8)
            nc.vector.tensor_copy(
                out=scales[h][:].rearrange("p g (t m) -> p g t m", t=PACK),
                in_=scale_raw[:, :, KPASS * h : KPASS * (h + 1)].rearrange("p g (m t) -> p g t m", t=PACK),
            )

        def order_w():
            nc.vector.tensor_copy(
                out=w_codes[:].bitcast(I32).rearrange("p g (t m i) -> p g m t i", t=PACK, i=2),
                in_=w_raw[:].bitcast(I32).rearrange("p g (m i t) -> p g m t i", t=PACK, i=2),
            )

        def group_da_on_vector(h):
            da_grouped[h] = ring("h_grouped", 2, [P, PACK * KPASS], BF16)
            nc.vector.tensor_copy(
                out=da_grouped[h][:].rearrange("p (t m i j) -> p m t i j", t=PACK, i=2, j=PACK),
                in_=da_raw[h][:].rearrange("p j (m i t) -> p m t i j", t=PACK, i=2),
            )

        def group_da_on_scalar(h):
            da_grouped[h] = ring("h_grouped", 2, [P, PACK * KPASS], BF16)
            nc.scalar.copy(
                out=da_grouped[h][:].rearrange("p (t m j) -> p t m j", t=PACK, j=PACK),
                in_=da_raw[h][:].rearrange("p j (m t) -> p t m j", t=PACK),
            )

        def quantize_da(h):
            da_codes[h] = held("da_codes%d" % h, [P, KPASS], U32)
            da_scales[h] = held("da_scales%d" % h, [P, KPASS], U8)
            nc.vector.quantize_mx(out=da_codes[h][:].bitcast(FP8X4), scales=da_scales[h][:], in_=da_grouped[h][:])

        def cast_fade():
            nc.scalar.copy(out=fade32[:], in_=vec["fade"][:, 0, :])

        def warm_up(count):
            idle = bank()
            for i in range(count):
                nc.tensor.matmul(idle[:], lhsT=zeros[:, :P], rhs=zeros[:], start=True, stop=True)

        z_ordered, prev_ordered = {}, {}

        def order_words(raw, copy):
            ordered = ring("staged", 4, [P, 2, PACK * P], F32)
            copy(
                out=ordered[:].rearrange("r u (m i) -> r m u i", i=2),
                in_=raw[:].bitcast(F32).rearrange("r a (m i u) -> r (a m) u i", i=2, u=2),
            )
            return ordered

        def order_z(c, key):
            z_ordered[c, key] = order_words(z_raw[c, key], on_vector)

        def order_prev(c):
            prev_ordered[c] = order_words(prev_raw[c], on_scalar)

        def words(raw, ordered, piece, u):
            if ordered is not None:
                return ordered[:, u, P * piece : P * (piece + 1)]
            flat = raw[:].bitcast(F32).rearrange("r a w -> r (a w)")
            return flat[:, 2 * P * piece + u : 2 * P * (piece + 1) : 2]

        z_banks, z_grouped, z_codes, z_scales = {}, {}, {}, {}

        def turn_z(c, g, half):
            z_banks[c, g, half] = bank()
            key = (c, ZA) if g == ZA else (c, half)
            for j in range(2):
                piece = 2 * half + j if g == ZA else 2 * j + g
                for u in range(2):
                    col = 2 * P * u + P * j
                    nc.tensor.transpose(
                        z_banks[c, g, half][:, col : col + P], words(z_raw[key], z_ordered.get(key), piece, u), ident[:]
                    )

        def copy_z(c, g, half, copy):
            if c not in z_grouped:
                z_grouped[c] = ring("z_grouped", 2, [P, 3 * PACK * CH], BF16)
            start = 2 * CH * g + CH * half
            copy(
                out=z_grouped[c][:].bitcast(F32)[:, start : start + CH].rearrange("p (r j u) -> p r j u", j=2, u=2),
                in_=z_banks[c, g, half][:].rearrange("p (u j r) -> p r j u", j=2, u=2),
            )

        def quantize_z(c, first, end):
            if c not in z_codes:
                z_codes[c] = ring("z_codes", 2, [P, 3 * CH], U32)
                z_scales[c] = ring("z_scales", 2, [P, 3 * CH], U8)
            cols = slice(CH * first, CH * end)
            nc.vector.quantize_mx(
                out=z_codes[c][:, cols].bitcast(FP8X4), scales=z_scales[c][:, cols],
                in_=z_grouped[c][:, PACK * CH * first : PACK * CH * end],
            )

        s_banks, squashed, h_grouped, h_codes, h_scales = {}, {}, {}, {}, {}

        def first_stage_pass(out, c, h, t, g, lo, hi):
            cols = slice(P * t, P * (t + 1))
            if g == ZA:
                lhsT, lhsT_scale = da_codes[h][:, cols].bitcast(FP8X4), da_scales[h][:, cols]
            else:
                lhsT, lhsT_scale = dp_codes[h][:, g, 2 * P * t : 2 * P * (t + 1)].bitcast(FP4X4), scales[h][:, g, cols]
            moving = slice(CH * g + lo, CH * g + hi)
            nc.tensor.matmul_mx(
                out=out, lhsT=lhsT, lhsT_scale=lhsT_scale,
                rhs=z_codes[c][:, moving].bitcast(FP8X4), rhs_scale=z_scales[c][:, moving],
                start=(g == 0), stop=(g == ZA),
            )

        def correlate_pass(c, h, t, g):
            if g == 0:
                s_banks[c, h, t] = bank()
            first_stage_pass(s_banks[c, h, t][:], c, h, t, g, 0, CH)

        def correlate(c, h, t):
            for g in range(ZA + 1):
                correlate_pass(c, h, t, g)

        def squash(c, h, t):
            if t == 0:
                squashed[c, h] = ring("squashed", 2, [P, PACK, CH], F32)
            nc.scalar.activation(out=squashed[c, h][:, t, :], in_=s_banks[c, h, t][:], func=ACT.Tanh)

        def weigh(c, h):
            h_grouped[c, h] = ring("h_grouped", 2, [P, PACK * CH], BF16)
            nc.vector.tensor_tensor(
                out=h_grouped[c, h][:].rearrange("p (n i t) -> p n t i", i=2, t=PACK),
                in0=squashed[c, h][:].rearrange("p t (n i) -> p n t i", i=2),
                in1=vec["cell_weight"][:, h, :].unsqueeze(1).unsqueeze(3).to_broadcast([P, HALF, PACK, 2]),
                op=ALU.mult,
            )

        def quantize_h(c, h, lo, hi):
            if lo == 0:
                h_codes[c, h] = ring("h_codes", 4, [P, CH], U32)
                h_scales[c, h] = ring("h_scales", 4, [P, CH], U8)
            nc.vector.quantize_mx(
                out=h_codes[c, h][:, lo:hi].bitcast(FP8X4), scales=h_scales[c, h][:, lo:hi],
                in_=h_grouped[c, h][:, PACK * lo : PACK * hi],
            )

        tile_banks = {}

        def correlate_tile(a):
            tile_banks[a] = bank()
            for t in range(PACK):
                for g in range(ZA + 1):
                    first_stage_pass(tile_banks[a][:, P * t : P * (t + 1)], LAST, 1, t, g, P * a, P * (a + 1))

        def squash_tile(a):
            if a == 0:
                squashed[LAST, 1] = ring("squashed", 2, [P, CH, PACK], F32)
            nc.scalar.activation(
                out=squashed[LAST, 1][:, P * a : P * (a + 1), :],
                in_=tile_banks[a][:].rearrange("p (t n) -> p n t", t=PACK), func=ACT.Tanh,
            )

        def weigh_tiles(lo, hi):
            if lo == 0:
                h_grouped[LAST, 1] = ring("h_grouped", 2, [P, PACK * CH], BF16)
            nc.vector.tensor_tensor(
                out=h_grouped[LAST, 1][:, PACK * lo : PACK * hi].rearrange("p (n t) -> p n t", t=PACK),
                in0=squashed[LAST, 1][:, lo:hi, :],
                in1=vec["cell_weight"][:, 1, :].unsqueeze(1).to_broadcast([P, hi - lo, PACK]),
                op=ALU.mult,
            )

        prev_banks, faded, f_banks, y_zones = {}, {}, {}, {}

        def turn_prev(c, u):
            prev_banks[c, u] = bank()
            for piece in range(PACK):
                nc.tensor.transpose(
                    prev_banks[c, u][:, P * piece : P * (piece + 1)], words(prev_raw[c], prev_ordered[c], piece, u), ident[:]
                )

        def fade_prev(c, t):
            if t == 0:
                faded[c] = ring("faded", 2, [P, PACK, CH], F32)
            pairs = prev_banks[c, t // 2][:].bitcast(BF16).rearrange("p (a j r e) -> p e a r j", a=2, j=2, e=2)
            nc.scalar.activation(
                out=faded[c][:, t, :].rearrange("p (a r j) -> p a r j", a=2, j=2), in_=pairs[:, t % 2],
                func=ACT.Identity, scale=fade32[:, t : t + 1], bias=vec["bias"][:, 0, t : t + 1],
            )

        def in_bank(lo, hi, b):
            width = hi - lo
            return [(CH // width * b + i, slice(width * i, width * (i + 1))) for i in range(CH // width)]

        def fuse(c, lo, hi, b):
            f_banks[c, lo, b] = bank()
            for t, place in in_bank(lo, hi, b):
                cols = slice(P * t, P * (t + 1))
                for h in range(2):
                    nc.tensor.matmul_mx(
                        out=f_banks[c, lo, b][:, place],
                        lhsT=w_codes[:, h, cols].bitcast(FP8X4), lhsT_scale=scales[1][W_ROW:P, h, cols],
                        rhs=h_codes[c, h][:, lo:hi].bitcast(FP8X4), rhs_scale=h_scales[c, h][:, lo:hi],
                        start=(h == 0), stop=(h == 1),
                    )

        def join(c, lo, hi, b):
            if c not in y_zones:
                y_zones[c] = ring("y_zones", 2, [P, PACK, CH], F32)
            for t, place in in_bank(lo, hi, b):
                nc.vector.scalar_tensor_tensor(
                    out=y_zones[c][:, t, lo:hi], in0=f_banks[c, lo, b][:, place],
                    scalar=vec["gain"][:, 0, t : t + 1], in1=faded[c][:, t, lo:hi], op0=ALU.mult, op1=ALU.add,
                )

        y_banks, y_grouped = {}, {}
        y_codes = held("y_codes", [P, T], U32)
        y_scales = held("y_scales", [P, T], U8)

        def turn_y(c, a):
            y_banks[c, a] = bank()
            for t in range(PACK):
                nc.tensor.transpose(y_banks[c, a][:, P * t : P * (t + 1)], y_zones[c][:, t, P * a : P * (a + 1)], ident[:])

        def copy_y(c, a):
            rows = ring("y_rows", 5, [P, N], F32)
            nc.scalar.copy(
                out=rows[:].rearrange("n (p t) -> n p t", t=PACK),
                in_=y_banks[c, a][:].rearrange("n (t p) -> n p t", t=PACK),
            )
            row = CH * c + P * a
            nc.sync.dma_start(out=out_0[row : row + P, :], in_=rows[:])

        def group_y(c, lo, hi, copy):
            if lo == 0:
                y_grouped[c] = ring("y_grouped", 2, [P, PACK * CH], BF16)
            copy(
                out=y_grouped[c][:, PACK * lo : PACK * hi].rearrange("p (n i t) -> p n t i", i=2, t=PACK),
                in_=y_zones[c][:, :, lo:hi].rearrange("p t (n i) -> p n t i", i=2),
            )

        def quantize_y(c, lo, hi):
            cols = slice(CH * c + lo, CH * c + hi)
            nc.vector.quantize_mx(
                out=y_codes[:, cols].bitcast(FP8X4), scales=y_scales[:, cols], in_=y_grouped[c][:, PACK * lo : PACK * hi]
            )

        def store_y_codes(c, lo, hi):
            cols = slice(CH * c + lo, CH * c + hi)
            nc.sync.dma_start(
                out=out_1[0, :, cols, :].rearrange("p m t -> p (m t)").bitcast(I32), in_=y_codes[:, cols].bitcast(I32)
            )

        def store_y_scales(lo, hi):
            for q in range(4):
                nc.sync.dma_start(
                    out=out_2[0, 4 * q : 4 * q + 4, lo:hi].bitcast(I32),
                    in_=y_scales[32 * q : 32 * q + 4, lo:hi].bitcast(I32),
                )


        warm_up(WARM_FIRST)
        order_scales(0)
        turn_z(0, 1, 0)
        order_dp(0)
        turn_z(0, 0, 0)
        warm_up(WARM_BETWEEN)
        copy_z(0, 1, 0, on_vector)
        turn_z(0, 0, 1)
        copy_z(0, 0, 0, on_scalar)
        turn_z(0, 1, 1)
        copy_z(0, 0, 1, on_vector)
        copy_z(0, 1, 1, on_scalar)
        quantize_z(0, 0, 1)
        turn_z(0, 2, 0)
        turn_z(0, 2, 1)
        quantize_z(0, 1, 2)
        group_da_on_vector(0)
        correlate_pass(0, 0, 0, 0)
        copy_z(0, 2, 0, on_scalar)
        correlate_pass(0, 0, 1, 0)
        correlate_pass(0, 0, 0, 1)
        correlate_pass(0, 0, 1, 1)
        copy_z(0, 2, 1, on_scalar)
        quantize_z(0, 2, 3)
        correlate_pass(0, 0, 2, 0)
        quantize_da(0)
        correlate_pass(0, 0, 3, 0)
        correlate_pass(0, 0, 2, 1)
        correlate_pass(0, 0, 0, 2)
        correlate_pass(0, 0, 3, 1)
        group_da_on_scalar(1)
        correlate_pass(0, 0, 1, 2)
        correlate_pass(0, 0, 2, 2)
        correlate_pass(0, 0, 3, 2)
        order_dp(1)
        turn_z(1, 0, 0)
        squash(0, 0, 0)
        squash(0, 0, 1)
        squash(0, 0, 2)
        turn_z(1, 1, 0)
        quantize_da(1)
        squash(0, 0, 3)
        order_scales(1)
        order_prev(0)
        correlate(0, 1, 0)
        turn_z(1, 1, 1)
        turn_z(1, 0, 1)
        squash(0, 1, 0)
        copy_z(1, 0, 0, on_vector)
        turn_prev(0, 0)
        correlate(0, 1, 1)
        cast_fade()
        copy_z(1, 1, 0, on_scalar)
        weigh(0, 0)
        fade_prev(0, 0)
        copy_z(1, 0, 1, on_scalar)
        turn_z(1, 2, 0)
        copy_z(1, 1, 1, on_vector)
        order_w()
        turn_z(1, 2, 1)
        quantize_z(1, 1, 2)
        fade_prev(0, 1)
        copy_z(1, 2, 0, on_vector)
        copy_z(1, 2, 1, on_scalar)
        turn_prev(0, 1)
        correlate(0, 1, 2)
        quantize_z(1, 0, 1)
        squash(0, 1, 1)
        correlate(0, 1, 3)
        quantize_z(1, 2, 3)
        quantize_h(0, 0, 0, CH)
        squash(0, 1, 2)
        fade_prev(0, 2)
        squash(0, 1, 3)
        fade_prev(0, 3)

        for c in range(1, LAST):
            correlate(c, 0, 0)
            order_prev(c)
            correlate(c, 0, 1)
            correlate(c, 0, 2)
            if c >= 2:
                copy_y(c - 2, 0)
            order_z(c + 1, 1)
            order_z(c + 1, 0)
            if c >= 2:
                copy_y(c - 2, 1)
                copy_y(c - 2, 2)
            squash(c, 0, 0)
            turn_z(c + 1, 1, 0)
            turn_z(c + 1, 0, 0)
            turn_z(c + 1, 1, 1)
            correlate(c, 0, 3)
            if c >= 2:
                copy_y(c - 2, 3)
            squash(c, 0, 1)
            squash(c, 0, 2)
            weigh(c - 1, 1)
            squash(c, 0, 3)
            copy_z(c + 1, 1, 0, on_scalar)
            order_z(c + 1, 2)
            copy_z(c + 1, 0, 0, on_scalar)
            turn_prev(c, 0)
            copy_z(c + 1, 1, 1, on_vector)
            quantize_h(c - 1, 1, 0, CH)
            turn_z(c + 1, 2, 0)
            fade_prev(c, 0)
            turn_z(c + 1, 0, 1)
            fade_prev(c, 1)
            copy_z(c + 1, 2, 0, on_scalar)
            correlate(c, 1, 0)
            fuse(c - 1, 0, CH, 0)
            weigh(c, 0)
            fuse(c - 1, 0, CH, 1)
            turn_prev(c, 1)
            turn_z(c + 1, 2, 1)
            join(c - 1, 0, CH, 0)
            join(c - 1, 0, CH, 1)
            copy_z(c + 1, 0, 1, on_scalar)
            squash(c, 1, 0)
            fuse(c - 1, 0, CH, 2)
            copy_z(c + 1, 2, 1, on_scalar)
            fuse(c - 1, 0, CH, 3)
            quantize_h(c, 0, 0, CH)
            quantize_z(c + 1, 0, 2)
            fade_prev(c, 2)
            correlate(c, 1, 1)
            join(c - 1, 0, CH, 2)
            correlate(c, 1, 2)
            correlate(c, 1, 3)
            fade_prev(c, 3)
            join(c - 1, 0, CH, 3)
            squash(c, 1, 1)
            quantize_z(c + 1, 2, 3)
            if c >= 2:
                quantize_y(c - 2, 0, CH)
                store_y_codes(c - 2, 0, CH)
            turn_y(c - 1, 0)
            turn_y(c - 1, 1)
            squash(c, 1, 2)
            squash(c, 1, 3)
            turn_y(c - 1, 2)
            turn_y(c - 1, 3)
            group_y(c - 1, 0, CH, on_vector)

        copy_y(LAST - 2, 0)
        order_prev(LAST)
        correlate(LAST, 0, 0)
        squash(LAST, 0, 0)
        correlate(LAST, 0, 1)
        copy_y(LAST - 2, 1)
        weigh(LAST - 1, 1)
        copy_y(LAST - 2, 2)
        correlate(LAST, 0, 2)
        quantize_h(LAST - 1, 1, 0, CH)
        correlate(LAST, 0, 3)
        turn_prev(LAST, 0)
        copy_y(LAST - 2, 3)
        turn_prev(LAST, 1)
        squash(LAST, 0, 1)
        quantize_y(LAST - 2, 0, CH)
        store_y_codes(LAST - 2, 0, CH)
        fuse(LAST - 1, 0, CH, 0)
        squash(LAST, 0, 2)
        fuse(LAST - 1, 0, CH, 1)
        join(LAST - 1, 0, CH, 0)
        fuse(LAST - 1, 0, CH, 2)
        join(LAST - 1, 0, CH, 1)
        squash(LAST, 0, 3)
        correlate_tile(0)
        join(LAST - 1, 0, CH, 2)
        fuse(LAST - 1, 0, CH, 3)
        fade_prev(LAST, 0)
        fade_prev(LAST, 1)
        fade_prev(LAST, 2)
        weigh(LAST, 0)
        join(LAST - 1, 0, CH, 3)
        fade_prev(LAST, 3)
        correlate_tile(1)
        squash_tile(0)
        quantize_h(LAST, 0, 0, CH)
        squash_tile(1)
        correlate_tile(2)
        squash_tile(2)
        turn_y(LAST - 1, 0)
        copy_y(LAST - 1, 0)
        correlate_tile(3)
        squash_tile(3)
        weigh_tiles(0, HALF)
        group_y(LAST - 1, 0, HALF, on_scalar)
        turn_y(LAST - 1, 1)
        turn_y(LAST - 1, 2)
        group_y(LAST - 1, HALF, CH, on_vector)
        turn_y(LAST - 1, 3)
        copy_y(LAST - 1, 1)
        quantize_h(LAST, 1, 0, HALF)
        weigh_tiles(HALF, CH)
        fuse(LAST, 0, HALF, 0)
        quantize_y(LAST - 1, 0, CH)
        quantize_h(LAST, 1, HALF, CH)
        fuse(LAST, 0, HALF, 1)
        fuse(LAST, HALF, CH, 0)
        copy_y(LAST - 1, 2)
        store_y_scales(0, LAST * CH)
        store_y_codes(LAST - 1, 0, CH)
        fuse(LAST, HALF, CH, 1)
        join(LAST, 0, HALF, 0)
        copy_y(LAST - 1, 3)
        join(LAST, 0, HALF, 1)
        join(LAST, HALF, CH, 0)
        turn_y(LAST, 0)
        join(LAST, HALF, CH, 1)
        turn_y(LAST, 1)
        copy_y(LAST, 0)
        turn_y(LAST, 2)
        copy_y(LAST, 1)
        turn_y(LAST, 3)
        group_y(LAST, 0, HALF, on_vector)
        quantize_y(LAST, 0, HALF)
        group_y(LAST, HALF, CH, on_vector)
        quantize_y(LAST, HALF, CH)
        copy_y(LAST, 2)
        copy_y(LAST, 3)
        store_y_codes(LAST, 0, HALF)
        store_y_codes(LAST, HALF, CH)
        store_y_scales(LAST * CH, T)
